import numpy as np
import ml_dtypes


def mxq(x, axis, fmt="e4m3"):
    dtype, down = {"e4m3": (ml_dtypes.float8_e4m3fn, 7), "e5m2": (ml_dtypes.float8_e5m2, 14)}[fmt]
    v = np.moveaxis(np.asarray(x, np.float32).astype(ml_dtypes.bfloat16).astype(np.float64), axis, -1)
    blocks = v.reshape(v.shape[:-1] + (-1, 32))
    amax = np.abs(blocks).max(-1, keepdims=True)
    byte = np.maximum(np.where(amax > 0, np.frexp(amax)[1] - 1 + 127, 0) - down, 1)
    scale = np.exp2(byte - 127.0)
    codes = (blocks / scale).astype(np.float32).astype(dtype).astype(np.float64)
    return np.moveaxis((codes * scale).reshape(v.shape), -1, axis)


WIDE = False


def mx_kscale(k):
    if not WIDE:
        return np.ones(k)
    levels = np.array([10, -10, 5, -5, 0])
    if k % 512:
        return np.exp2(np.random.permutation(np.resize(levels, k // 32))).repeat(32)
    a = np.empty((k // 512, 16))
    for p in range(k // 512):
        a[p, :8] = np.random.permutation(np.resize(levels, 8))
        for g in range(8):
            far = levels[np.abs(levels - a[p, g]) >= 10]
            a[p, g + 8] = far[np.random.randint(len(far))]
    return np.exp2(a.ravel()).repeat(32)


def f64(x):
    return np.asarray(x).astype(np.float64)


def striped(idx):
    return np.tile(idx.reshape(-1, 16).T, (8, 1)).astype(np.uint16)


def unstriped(offs):
    return offs[:16].T.reshape(-1).astype(np.int64)


def gelu(v):
    return 0.5 * v * (1.0 + np.tanh(np.sqrt(2.0 / np.pi) * (v + 0.044715 * v**3)))


K, T, D, S, V, N = 1536, 1024, 16, 512, 32, 512


def setup_inputs():
    n = np.random.standard_normal
    s = mx_kscale(K)[:, None]
    return {
        "xT": (n((K, T)) * s).astype(np.float32),
        "w": (n((K, N)) / np.sqrt(K) / s).astype(np.float32),
        "b": (0.3 * n((N, 1))).astype(np.float32),
        "offs": striped(np.random.permutation(T)[:S]),
    }


def reference(xT, w, b, offs):
    idx = unstriped(offs)
    xq = mxq(f64(xT)[:, idx], 0, "e4m3")
    y = mxq(f64(w), 0, "e4m3").T @ xq
    y = gelu(y + f64(b))
    return y.reshape(N, V, D).max(axis=2)

@@ -1,0 +1,191 @@
+from contextlib import ExitStack
+
+import concourse.mybir as mybir
+from concourse.masks import make_identity
+
+K, T, D, S, V, N = 1536, 1024, 16, 512, 32, 512
+FLOPS = 2 * K * N * S
+
+F32 = mybir.dt.float32
+BF16 = mybir.dt.bfloat16
+U32 = mybir.dt.uint32
+I32 = mybir.dt.int32
+U16 = mybir.dt.uint16
+U8 = mybir.dt.uint8
+FP8X4 = mybir.dt.float8_e4m3fn_x4
+COPY = mybir.ActivationFunctionType.Copy
+GELU = mybir.ActivationFunctionType.Gelu_apprx_tanh
+
+P = 128
+PACK = 4
+K_PASS = P * PACK
+PASSES = K // K_PASS
+M_TILES = N // P
+
+LOADS = [["x",0,0,0,512],["x",0,0,512,1024],["x",0,1,0,512],["x",0,1,512,1024],["x",1,0,0,512],["x",1,0,512,1024],["x",1,1,0,512],["x",1,1,512,1024],["x",2,0,0,512],["x",2,0,512,1024],["x",2,1,0,512],["x",2,1,512,1024],["w",0],["w",1],["w",2],["w",3],["w",4],["w",5],["w",6]]
+STEPS = [["cx",0,0],["cx",1,1],["cw",2],["cx",0,1],["g",0,1],["cx",1,0],["cw",0],["g",0,0],["g",1,0],["cw",3],["cw",1],["il",0],["cw",5],["qw",5],["cx",2,1],["g",1,1],["qw",1],["cx",2,0],["il",1],["qx",0],["qw",0],["cw",6],["qw",3],["g",2,0],["mm",0],["g",2,1],["qx",1],["il",2],["mm",1],["mm",3],["qx",2],["qw",2],["mm",2],["wm"],["cw",4],["gelu",0],["gelu",1],["qw",6],["qw",4],["mm",6],["mm",4],["max",0],["mm",5],["gelu",3],["gelu",2],["max",2],["max",1],["max",3]]
+N_SPLIT = [1,1,1,2]
+WARM = 1
+X_SPLIT = [[["scalar",0,960],["vector",960,1024]],[["vector",0,192],["scalar",192,1024]],[["vector",0,704],["scalar",704,1024]],[["scalar",0,1024],["vector",1024,1024]],[["vector",0,576],["scalar",576,1024]],[["scalar",0,1024],["vector",1024,1024]]]
+W_PIECES = [[0,0,256,[["scalar",0,256],["vector",256,256]]],[1,0,256,[["scalar",0,256],["vector",256,256]]],[2,0,256,[["scalar",0,160],["vector",160,256]]],[0,256,512,[["scalar",0,224],["vector",224,256]]],[1,256,512,[["scalar",0,128],["vector",128,256]]],[2,256,384,[["scalar",0,96],["vector",96,128]]],[2,384,512,[["scalar",0,0],["vector",0,128]]]]
+TAIL_PARTS = [1,1,2,2]
+
+
+def tile_picked_pool_lin_gelu_sub_e_kernel(tc, xT, w, b, offs, out):
+    nc = tc.nc
+    with ExitStack() as ctx:
+        keep = ctx.enter_context(tc.tile_pool(name="keep", bufs=1))
+        psum = ctx.enter_context(tc.psum_pool(name="psum", bufs=1))
+
+        def rounded_copy(engine, dst, src):
+            if engine == "scalar":
+                nc.scalar.activation(out=dst, in_=src, func=COPY)
+            else:
+                nc.vector.tensor_copy(out=dst, in_=src)
+
+        warm = keep.tile([P, 8], F32, name="warm")
+        nc.gpsimd.memset(warm[:], 0.0)
+        warm_out = keep.tile([P, 8], F32, name="warm_out")
+        nc.scalar.activation(out=warm_out[:], in_=warm[:], func=GELU)
+
+        ident = keep.tile([P, P], F32, name="ident")
+        make_identity(nc, ident[:])
+        bias_rows = keep.tile([P, P], F32, name="bias_rows")
+        nc.gpsimd.memset(bias_rows[:], 0.0)
+
+        x_raw, w_raw = {}, {}
+        offsets = keep.tile([P, S // 16], U16, name="offsets")
+        for n, load in enumerate(LOADS):
+            if load[0] == "x":
+                a, u, t0, t1 = load[1:]
+                rows = xT[a * K_PASS : (a + 1) * K_PASS, :].rearrange("(p j) t -> p j t", j=PACK)
+                raw = keep.tile([P, 2, t1 - t0], F32, name=f"x_raw{a}_{u}_{t0}")
+                nc.sync.dma_start(out=raw[:], in_=rows[:, 2 * u : 2 * u + 2, t0:t1])
+                x_raw[a, u, t0, t1] = raw
+            else:
+                a, c0, c1, shares = W_PIECES[load[1]]
+                raw = keep.tile([P, PACK, c1 - c0], F32, name=f"w_raw{a}_{c0}")
+                rows = w[a * K_PASS : (a + 1) * K_PASS, :].rearrange("(p j) n -> p j n", j=PACK)
+                nc.sync.dma_start(out=raw[:], in_=rows[:, :, c0:c1])
+                w_raw[load[1]] = raw
+            if n == 1:
+                nc.sync.dma_start(offsets[:], offs)
+            if n == 3:
+                nc.sync.dma_start(out=bias_rows[0:M_TILES, :], in_=b.rearrange("(c p) o -> c (p o)", p=P))
+
+        bias_bank = psum.tile([P, P], F32, name="bias_bank")
+        nc.tensor.transpose(bias_bank[:], bias_rows[:], ident[:])
+        bias = keep.tile([P, M_TILES], F32, name="bias")
+        nc.vector.tensor_copy(out=bias[:], in_=bias_bank[:, 0:M_TILES])
+
+        pairs = {(a, u): keep.tile([P, T, 2], BF16, name=f"pairs{a}_{u}") for a in range(PASSES) for u in range(2)}
+        picked = [keep.tile([P, 2, S, 2], BF16, name=f"picked{a}") for a in range(PASSES)]
+        x_grouped = [keep.tile([P, S * PACK], BF16, name=f"x_grouped{a}", align_bytes=64) for a in range(PASSES)]
+        x_codes = [keep.tile([P, S], U32, name=f"x_codes{a}", align_bytes=64) for a in range(PASSES)]
+        x_scales = [keep.tile([P, S], U8, name=f"x_scales{a}", align_bytes=64) for a in range(PASSES)]
+        w_grouped, w_codes, w_scales = [], [], []
+        for a, c0, c1, shares in W_PIECES:
+            w_grouped.append(keep.tile([P, c1 - c0, PACK], BF16, name=f"w_grouped{a}_{c0}", align_bytes=64))
+            w_codes.append(keep.tile([P, c1 - c0], U32, name=f"w_codes{a}_{c0}", align_bytes=64))
+            w_scales.append(keep.tile([P, c1 - c0], U8, name=f"w_scales{a}_{c0}", align_bytes=64))
+        acc = {
+            (m, h): psum.tile([P, S // N_SPLIT[m]], F32, name=f"acc{m}_{h}")
+            for m in range(M_TILES)
+            for h in range(N_SPLIT[m])
+        }
+        passes_done = [0] * M_TILES
+        y = {}
+        pooled = [keep.tile([P, V], F32, name=f"pooled{m}") for m in range(M_TILES)]
+
+        for step in STEPS:
+            kind = step[0]
+            if kind == "cx":
+                a, u = step[1:]
+                for (a2, u2, t0, t1), raw in x_raw.items():
+                    if (a2, u2) == (a, u):
+                        for engine, s0, s1 in X_SPLIT[2 * a + u]:
+                            lo, hi = max(s0, t0), min(s1, t1)
+                            if lo < hi:
+                                src = raw[:, :, lo - t0 : hi - t0].rearrange("p e t -> p t e")
+                                rounded_copy(engine, pairs[a, u][:, lo:hi, :], src)
+            elif kind == "g":
+                a, u = step[1:]
+                window = pairs[a, u][:].rearrange("p t e -> p (t e)").bitcast(U32)
+                dense = picked[a][:, u, :, :].rearrange("p s e -> p (s e)").bitcast(U32)
+                nc.vector.tensor_copy(out=dense, in_=window.indirect(offsets[:]))
+            elif kind == "il":
+                a = step[1]
+                words = picked[a][:].rearrange("p u s e -> p (u s e)").bitcast(I32)
+                nc.vector.tensor_copy(
+                    out=x_grouped[a][:].bitcast(I32).rearrange("p (s u) -> p s u", u=2),
+                    in_=words.rearrange("p (u s) -> p s u", u=2),
+                )
+            elif kind == "qx":
+                a = step[1]
+                nc.vector.quantize_mx(out=x_codes[a][:].bitcast(FP8X4), scales=x_scales[a][:], in_=x_grouped[a][:])
+            elif kind == "cw":
+                i = step[1]
+                for engine, s0, s1 in W_PIECES[i][3]:
+                    if s0 < s1:
+                        rounded_copy(
+                            engine,
+                            w_grouped[i][:, s0:s1, :].rearrange("p (c i) j -> p c j i", i=4),
+                            w_raw[i][:, :, s0:s1].rearrange("p j (c i) -> p c j i", i=4),
+                        )
+            elif kind == "qw":
+                i = step[1]
+                nc.vector.quantize_mx(
+                    out=w_codes[i][:].bitcast(FP8X4),
+                    scales=w_scales[i][:],
+                    in_=w_grouped[i][:].rearrange("p c j -> p (c j)"),
+                )
+            elif kind == "wm":
+                spare = psum.tile([P, S], F32, name="spare")
+                for r in range(3):
+                    nc.tensor.matmul_mx(
+                        out=spare[:],
+                        lhsT=x_codes[WARM][:, 0:P].bitcast(FP8X4),
+                        lhsT_scale=x_scales[WARM][:, 0:P],
+                        rhs=x_codes[WARM][:].bitcast(FP8X4),
+                        rhs_scale=x_scales[WARM][:],
+                        start=True,
+                        stop=True,
+                    )
+            elif kind == "mm":
+                i = step[1]
+                a, c0, c1 = W_PIECES[i][:3]
+                for m in range(c0 // P, c1 // P):
+                    cols = slice(m * P - c0, (m + 1) * P - c0)
+                    for h in range(N_SPLIT[m]):
+                        picks = slice(h * S // N_SPLIT[m], (h + 1) * S // N_SPLIT[m])
+                        nc.tensor.matmul_mx(
+                            out=acc[m, h][:],
+                            lhsT=w_codes[i][:, cols].bitcast(FP8X4),
+                            lhsT_scale=w_scales[i][:, cols],
+                            rhs=x_codes[a][:, picks].bitcast(FP8X4),
+                            rhs_scale=x_scales[a][:, picks],
+                            start=(passes_done[m] == 0),
+                            stop=(passes_done[m] == PASSES - 1),
+                        )
+                    passes_done[m] += 1
+            elif kind == "gelu":
+                m = step[1]
+                parts = TAIL_PARTS[m]
+                width = S // parts
+                for h in range(parts):
+                    g, n0 = divmod(h * width, S // N_SPLIT[m])
+                    y[m, h] = keep.tile([P, width], F32, name=f"y{m}_{h}")
+                    nc.scalar.activation(
+                        out=y[m, h][:], in_=acc[m, g][:, n0 : n0 + width], func=GELU, bias=bias[:, m : m + 1]
+                    )
+            else:
+                m = step[1]
+                parts = TAIL_PARTS[m]
+                for h in range(parts):
+                    nc.vector.tensor_reduce(
+                        out=pooled[m][:, h * V // parts : (h + 1) * V // parts],
+                        in_=y[m, h][:].rearrange("p (v d) -> p v d", d=D),
+                        axis=mybir.AxisListType.X,
+                        op=mybir.AluOpType.max,
+                    )
+                nc.sync.dma_start(out=out[m * P : (m + 1) * P, :], in_=pooled[m][:])

@@ -22,12 +22,14 @@ K_PASS = P * PACK
 PASSES = K // K_PASS
 M_TILES = N // P
 
-LOADS = [["x",0,0,0,512],["x",0,0,512,1024],["x",0,1,0,512],["x",0,1,512,1024],["x",1,0,0,512],["x",1,0,512,1024],["x",1,1,0,512],["x",1,1,512,1024],["x",2,0,0,512],["x",2,0,512,1024],["x",2,1,0,512],["x",2,1,512,1024],["w",0],["w",1],["w",2],["w",3],["w",4],["w",5],["w",6]]
-STEPS = [["cx",0,0],["cx",1,1],["cw",2],["cx",0,1],["g",0,1],["cx",1,0],["cw",0],["g",0,0],["g",1,0],["cw",3],["cw",1],["il",0],["cw",5],["qw",5],["cx",2,1],["g",1,1],["qw",1],["cx",2,0],["il",1],["qx",0],["qw",0],["cw",6],["qw",3],["g",2,0],["mm",0],["g",2,1],["qx",1],["il",2],["mm",1],["mm",3],["qx",2],["qw",2],["mm",2],["wm"],["cw",4],["gelu",0],["gelu",1],["qw",6],["qw",4],["mm",6],["mm",4],["max",0],["mm",5],["gelu",3],["gelu",2],["max",2],["max",1],["max",3]]
+LOADS = [["x",0,0,0,1024],["x",0,1,0,1024],["x",1,0,0,1024],["x",1,1,0,1024],["x",2,0,0,1024],["x",2,1,0,512],["x",2,1,512,1024],["w",0],["w",1],["w",2],["w",3],["w",4],["w",5],["w",6],["w",7]]
+STEPS = [["cx",0,0],["cx",1,1],["cw",0],["cx",1,0],["cx",0,1],["g",0,1],["g",1,0],["g",1,1],["cw",3],["il",1],["g",0,0],["il",0],["cx",2,1],["cx",2,0],["qx",1],["qx",0],["cw",4],["cw",2],["qw",0],["qw",2],["cw",1],["wm",1],["mm",0],["g",2,0],["qw",3],["wm",2],["g",2,1],["qw",1],["il",2],["wm",0],["qx",2],["mm",1],["mm",2],["qw",4],["mm",3],["cw",7],["cw",6],["qw",6],["cw",5],["gelu",0],["mm",4],["gelu",1],["max",1],["qw",5],["mm",5],["qw",7],["mm",6],["gelu",2],["max",0],["mm",7],["gelu",3],["max",3],["max",2]]
 N_SPLIT = [1,1,1,2]
-WARM = 1
-X_SPLIT = [[["scalar",0,960],["vector",960,1024]],[["vector",0,192],["scalar",192,1024]],[["vector",0,704],["scalar",704,1024]],[["scalar",0,1024],["vector",1024,1024]],[["vector",0,576],["scalar",576,1024]],[["scalar",0,1024],["vector",1024,1024]]]
-W_PIECES = [[0,0,256,[["scalar",0,256],["vector",256,256]]],[1,0,256,[["scalar",0,256],["vector",256,256]]],[2,0,256,[["scalar",0,160],["vector",160,256]]],[0,256,512,[["scalar",0,224],["vector",224,256]]],[1,256,512,[["scalar",0,128],["vector",128,256]]],[2,256,384,[["scalar",0,96],["vector",96,128]]],[2,384,512,[["scalar",0,0],["vector",0,128]]]]
+WARM = [["qx",0],["qx",1],["qx",1]]
+W_LOADS = [[0,0,256],[1,0,256],[2,0,256],[0,256,512],[1,256,384],[2,256,384],[1,384,512],[2,384,512]]
+X_PARTS = [2,2,2]
+X_SPLIT = [[["scalar",0,320],["vector",320,1024]],[["vector",0,640],["scalar",640,1024]],[["scalar",0,768],["vector",768,1024]],[["vector",0,384],["scalar",384,1024]],[["scalar",0,704],["vector",704,1024]],[["vector",0,0],["scalar",0,1024]]]
+W_PIECES = [[0,0,256,[["scalar",0,96],["vector",96,256]]],[1,0,256,[["scalar",0,256],["vector",256,256]]],[2,0,256,[["scalar",0,256],["vector",256,256]]],[0,256,512,[["scalar",0,256],["vector",256,256]]],[1,256,384,[["scalar",0,64],["vector",64,128]]],[2,256,384,[["scalar",0,128],["vector",128,128]]],[1,384,512,[["scalar",0,96],["vector",96,128]]],[2,384,512,[["scalar",0,0],["vector",0,128]]]]
 TAIL_PARTS = [1,1,2,2]
 
 
@@ -63,14 +65,14 @@ def tile_picked_pool_lin_gelu_sub_e_kernel(tc, xT, w, b, offs, out):
                 nc.sync.dma_start(out=raw[:], in_=rows[:, 2 * u : 2 * u + 2, t0:t1])
                 x_raw[a, u, t0, t1] = raw
             else:
-                a, c0, c1, shares = W_PIECES[load[1]]
+                a, c0, c1 = W_LOADS[load[1]]
                 raw = keep.tile([P, PACK, c1 - c0], F32, name=f"w_raw{a}_{c0}")
                 rows = w[a * K_PASS : (a + 1) * K_PASS, :].rearrange("(p j) n -> p j n", j=PACK)
                 nc.sync.dma_start(out=raw[:], in_=rows[:, :, c0:c1])
-                w_raw[load[1]] = raw
-            if n == 1:
+                w_raw[a, c0, c1] = raw
+            if n == 0:
                 nc.sync.dma_start(offsets[:], offs)
-            if n == 3:
+            if n == 1:
                 nc.sync.dma_start(out=bias_rows[0:M_TILES, :], in_=b.rearrange("(c p) o -> c (p o)", p=P))
 
         bias_bank = psum.tile([P, P], F32, name="bias_bank")
@@ -93,6 +95,7 @@ def tile_picked_pool_lin_gelu_sub_e_kernel(tc, xT, w, b, offs, out):
             for m in range(M_TILES)
             for h in range(N_SPLIT[m])
         }
+        spare = psum.tile([P, S], F32, name="spare")
         passes_done = [0] * M_TILES
         y = {}
         pooled = [keep.tile([P, V], F32, name=f"pooled{m}") for m in range(M_TILES)]
@@ -110,28 +113,42 @@ def tile_picked_pool_lin_gelu_sub_e_kernel(tc, xT, w, b, offs, out):
                                 rounded_copy(engine, pairs[a, u][:, lo:hi, :], src)
             elif kind == "g":
                 a, u = step[1:]
+                parts = X_PARTS[a] if u == 1 else 1
                 window = pairs[a, u][:].rearrange("p t e -> p (t e)").bitcast(U32)
                 dense = picked[a][:, u, :, :].rearrange("p s e -> p (s e)").bitcast(U32)
-                nc.vector.tensor_copy(out=dense, in_=window.indirect(offsets[:]))
+                for h in range(parts):
+                    s0, s1 = h * S // parts, (h + 1) * S // parts
+                    nc.vector.tensor_copy(out=dense[:, s0:s1], in_=window.indirect(offsets[:, s0 // 16 : s1 // 16]))
             elif kind == "il":
                 a = step[1]
-                words = picked[a][:].rearrange("p u s e -> p (u s e)").bitcast(I32)
-                nc.vector.tensor_copy(
-                    out=x_grouped[a][:].bitcast(I32).rearrange("p (s u) -> p s u", u=2),
-                    in_=words.rearrange("p (u s) -> p s u", u=2),
-                )
+                parts = X_PARTS[a]
+                words = picked[a][:].rearrange("p u s e -> p (u s e)").bitcast(I32).rearrange("p (u s) -> p s u", u=2)
+                side_by_side = x_grouped[a][:].bitcast(I32).rearrange("p (s u) -> p s u", u=2)
+                for h in range(parts):
+                    s0, s1 = h * S // parts, (h + 1) * S // parts
+                    nc.vector.tensor_copy(out=side_by_side[:, s0:s1, :], in_=words[:, s0:s1, :])
             elif kind == "qx":
                 a = step[1]
-                nc.vector.quantize_mx(out=x_codes[a][:].bitcast(FP8X4), scales=x_scales[a][:], in_=x_grouped[a][:])
+                parts = X_PARTS[a]
+                for h in range(parts):
+                    s0, s1 = h * S // parts, (h + 1) * S // parts
+                    nc.vector.quantize_mx(
+                        out=x_codes[a][:, s0:s1].bitcast(FP8X4),
+                        scales=x_scales[a][:, s0:s1],
+                        in_=x_grouped[a][:, PACK * s0 : PACK * s1],
+                    )
             elif kind == "cw":
                 i = step[1]
-                for engine, s0, s1 in W_PIECES[i][3]:
-                    if s0 < s1:
-                        rounded_copy(
-                            engine,
-                            w_grouped[i][:, s0:s1, :].rearrange("p (c i) j -> p c j i", i=4),
-                            w_raw[i][:, :, s0:s1].rearrange("p j (c i) -> p c j i", i=4),
-                        )
+                a, c0 = W_PIECES[i][:2]
+                for (a2, l0, l1), raw in w_raw.items():
+                    if a2 == a and l0 <= c0 < l1:
+                        for engine, s0, s1 in W_PIECES[i][3]:
+                            if s0 < s1:
+                                rounded_copy(
+                                    engine,
+                                    w_grouped[i][:, s0:s1, :].rearrange("p (c i) j -> p c j i", i=4),
+                                    raw[:, :, c0 - l0 + s0 : c0 - l0 + s1].rearrange("p j (c i) -> p c j i", i=4),
+                                )
             elif kind == "qw":
                 i = step[1]
                 nc.vector.quantize_mx(
@@ -140,17 +157,18 @@ def tile_picked_pool_lin_gelu_sub_e_kernel(tc, xT, w, b, offs, out):
                     in_=w_grouped[i][:].rearrange("p c j -> p (c j)"),
                 )
             elif kind == "wm":
-                spare = psum.tile([P, S], F32, name="spare")
-                for r in range(3):
-                    nc.tensor.matmul_mx(
-                        out=spare[:],
-                        lhsT=x_codes[WARM][:, 0:P].bitcast(FP8X4),
-                        lhsT_scale=x_scales[WARM][:, 0:P],
-                        rhs=x_codes[WARM][:].bitcast(FP8X4),
-                        rhs_scale=x_scales[WARM][:],
-                        start=True,
-                        stop=True,
-                    )
+                source, i = WARM[step[1]]
+                a = i if source == "qx" else 0
+                codes, scales = (x_codes[i], x_scales[i]) if source == "qx" else (w_codes[i], w_scales[i])
+                nc.tensor.matmul_mx(
+                    out=spare[:],
+                    lhsT=codes[:, 0:P].bitcast(FP8X4),
+                    lhsT_scale=scales[:, 0:P],
+                    rhs=x_codes[a][:].bitcast(FP8X4),
+                    rhs_scale=x_scales[a][:],
+                    start=True,
+                    stop=True,
+                )
             elif kind == "mm":
                 i = step[1]
                 a, c0, c1 = W_PIECES[i][:3]

@@ -21,16 +21,48 @@ PACK = 4
 K_PASS = P * PACK
 PASSES = K // K_PASS
 M_TILES = N // P
+STRIPE = 16
+RUN = 4
 
-LOADS = [["x",0,0,0,1024],["x",0,1,0,1024],["x",1,0,0,1024],["x",1,1,0,1024],["x",2,0,0,1024],["x",2,1,0,512],["x",2,1,512,1024],["w",0],["w",1],["w",2],["w",3],["w",4],["w",5],["w",6],["w",7]]
-STEPS = [["cx",0,0],["cx",1,1],["cw",0],["cx",1,0],["cx",0,1],["g",0,1],["g",1,0],["g",1,1],["cw",3],["il",1],["g",0,0],["il",0],["cx",2,1],["cx",2,0],["qx",1],["qx",0],["cw",4],["cw",2],["qw",0],["qw",2],["cw",1],["wm",1],["mm",0],["g",2,0],["qw",3],["wm",2],["g",2,1],["qw",1],["il",2],["wm",0],["qx",2],["mm",1],["mm",2],["qw",4],["mm",3],["cw",7],["cw",6],["qw",6],["cw",5],["gelu",0],["mm",4],["gelu",1],["max",1],["qw",5],["mm",5],["qw",7],["mm",6],["gelu",2],["max",0],["mm",7],["gelu",3],["max",3],["max",2]]
-N_SPLIT = [1,1,1,2]
-WARM = [["qx",0],["qx",1],["qx",1]]
-W_LOADS = [[0,0,256],[1,0,256],[2,0,256],[0,256,512],[1,256,384],[2,256,384],[1,384,512],[2,384,512]]
-X_PARTS = [2,2,2]
-X_SPLIT = [[["scalar",0,320],["vector",320,1024]],[["vector",0,640],["scalar",640,1024]],[["scalar",0,768],["vector",768,1024]],[["vector",0,384],["scalar",384,1024]],[["scalar",0,704],["vector",704,1024]],[["vector",0,0],["scalar",0,1024]]]
-W_PIECES = [[0,0,256,[["scalar",0,96],["vector",96,256]]],[1,0,256,[["scalar",0,256],["vector",256,256]]],[2,0,256,[["scalar",0,256],["vector",256,256]]],[0,256,512,[["scalar",0,256],["vector",256,256]]],[1,256,384,[["scalar",0,64],["vector",64,128]]],[2,256,384,[["scalar",0,128],["vector",128,128]]],[1,384,512,[["scalar",0,96],["vector",96,128]]],[2,384,512,[["scalar",0,0],["vector",0,128]]]]
-TAIL_PARTS = [1,1,2,2]
+X_LOADS = [(0, 0, 0, T), (0, 1, 0, T), (1, 0, 0, T), (1, 1, 0, T), (2, 0, 0, T), (2, 1, 0, T // 2), (2, 1, T // 2, T)]
+
+X_SHARES = [
+    [("scalar", 0, 320), ("vector", 320, 1024)],
+    [("vector", 0, 640), ("scalar", 640, 1024)],
+    [("scalar", 0, 768), ("vector", 768, 1024)],
+    [("vector", 0, 384), ("scalar", 384, 1024)],
+    [("scalar", 0, 704), ("vector", 704, 1024)],
+    [("scalar", 0, 512)],
+    [("scalar", 0, 512)],
+]
+
+W_LOADS = [
+    (0, 0, 256),
+    (1, 0, 256),
+    (2, 0, 256),
+    (0, 256, 512),
+    (1, 256, 384),
+    (2, 256, 384),
+    (1, 384, 512),
+    (2, 384, 512),
+]
+
+W_SCALAR_COLUMNS = [96, 256, 256, 256, 64, 128, 96, 0]
+
+LIST_HALVES = [slice(0, S // 2), slice(S // 2, S)]
+WHOLE_LIST = [slice(0, S)]
+
+PSUM_GROUPS = [WHOLE_LIST, WHOLE_LIST, WHOLE_LIST, LIST_HALVES]
+EPILOGUE_PARTS = [WHOLE_LIST, WHOLE_LIST, LIST_HALVES, LIST_HALVES]
+
+WARM_UP_PASSES = 3
+
+
+def round_to_bf16(nc, engine, dst, src):
+    if engine == "scalar":
+        nc.scalar.activation(out=dst, in_=src, func=COPY)
+    else:
+        nc.vector.tensor_copy(out=dst, in_=src)
 
 
 def tile_picked_pool_lin_gelu_sub_e_kernel(tc, xT, w, b, offs, out):
@@ -39,171 +71,142 @@ def tile_picked_pool_lin_gelu_sub_e_kernel(tc, xT, w, b, offs, out):
         keep = ctx.enter_context(tc.tile_pool(name="keep", bufs=1))
         psum = ctx.enter_context(tc.psum_pool(name="psum", bufs=1))
 
-        def rounded_copy(engine, dst, src):
-            if engine == "scalar":
-                nc.scalar.activation(out=dst, in_=src, func=COPY)
-            else:
-                nc.vector.tensor_copy(out=dst, in_=src)
-
-        warm = keep.tile([P, 8], F32, name="warm")
-        nc.gpsimd.memset(warm[:], 0.0)
-        warm_out = keep.tile([P, 8], F32, name="warm_out")
-        nc.scalar.activation(out=warm_out[:], in_=warm[:], func=GELU)
-
-        ident = keep.tile([P, P], F32, name="ident")
-        make_identity(nc, ident[:])
         bias_rows = keep.tile([P, P], F32, name="bias_rows")
         nc.gpsimd.memset(bias_rows[:], 0.0)
+        nc.scalar.dma_start(out=bias_rows[0:M_TILES, :], in_=b.rearrange("(m p) o -> m (p o)", p=P))
 
-        x_raw, w_raw = {}, {}
-        offsets = keep.tile([P, S // 16], U16, name="offsets")
-        for n, load in enumerate(LOADS):
-            if load[0] == "x":
-                a, u, t0, t1 = load[1:]
-                rows = xT[a * K_PASS : (a + 1) * K_PASS, :].rearrange("(p j) t -> p j t", j=PACK)
-                raw = keep.tile([P, 2, t1 - t0], F32, name=f"x_raw{a}_{u}_{t0}")
-                nc.sync.dma_start(out=raw[:], in_=rows[:, 2 * u : 2 * u + 2, t0:t1])
-                x_raw[a, u, t0, t1] = raw
-            else:
-                a, c0, c1 = W_LOADS[load[1]]
-                raw = keep.tile([P, PACK, c1 - c0], F32, name=f"w_raw{a}_{c0}")
-                rows = w[a * K_PASS : (a + 1) * K_PASS, :].rearrange("(p j) n -> p j n", j=PACK)
-                nc.sync.dma_start(out=raw[:], in_=rows[:, :, c0:c1])
-                w_raw[a, c0, c1] = raw
-            if n == 0:
-                nc.sync.dma_start(offsets[:], offs)
-            if n == 1:
-                nc.sync.dma_start(out=bias_rows[0:M_TILES, :], in_=b.rearrange("(c p) o -> c (p o)", p=P))
+        zeros = keep.tile([P, 8], F32, name="zeros")
+        nc.gpsimd.memset(zeros[:], 0.0)
+        gelu_of_zeros = keep.tile([P, 8], F32, name="gelu_of_zeros")
+        nc.scalar.activation(out=gelu_of_zeros[:], in_=zeros[:], func=GELU)
 
+        identity = keep.tile([P, P], F32, name="identity")
+        make_identity(nc, identity[:])
         bias_bank = psum.tile([P, P], F32, name="bias_bank")
-        nc.tensor.transpose(bias_bank[:], bias_rows[:], ident[:])
+        nc.tensor.transpose(bias_bank[:], bias_rows[:], identity[:])
         bias = keep.tile([P, M_TILES], F32, name="bias")
         nc.vector.tensor_copy(out=bias[:], in_=bias_bank[:, 0:M_TILES])
 
-        pairs = {(a, u): keep.tile([P, T, 2], BF16, name=f"pairs{a}_{u}") for a in range(PASSES) for u in range(2)}
-        picked = [keep.tile([P, 2, S, 2], BF16, name=f"picked{a}") for a in range(PASSES)]
-        x_grouped = [keep.tile([P, S * PACK], BF16, name=f"x_grouped{a}", align_bytes=64) for a in range(PASSES)]
-        x_codes = [keep.tile([P, S], U32, name=f"x_codes{a}", align_bytes=64) for a in range(PASSES)]
-        x_scales = [keep.tile([P, S], U8, name=f"x_scales{a}", align_bytes=64) for a in range(PASSES)]
-        w_grouped, w_codes, w_scales = [], [], []
-        for a, c0, c1, shares in W_PIECES:
-            w_grouped.append(keep.tile([P, c1 - c0, PACK], BF16, name=f"w_grouped{a}_{c0}", align_bytes=64))
-            w_codes.append(keep.tile([P, c1 - c0], U32, name=f"w_codes{a}_{c0}", align_bytes=64))
-            w_scales.append(keep.tile([P, c1 - c0], U8, name=f"w_scales{a}_{c0}", align_bytes=64))
-        acc = {
-            (m, h): psum.tile([P, S // N_SPLIT[m]], F32, name=f"acc{m}_{h}")
-            for m in range(M_TILES)
-            for h in range(N_SPLIT[m])
-        }
-        spare = psum.tile([P, S], F32, name="spare")
-        passes_done = [0] * M_TILES
-        y = {}
-        pooled = [keep.tile([P, V], F32, name=f"pooled{m}") for m in range(M_TILES)]
+        offsets = keep.tile([P, S // STRIPE], U16, name="offsets")
+        x_raw = []
+        for a, u, t0, t1 in X_LOADS:
+            rows = xT[a * K_PASS : (a + 1) * K_PASS, :].rearrange("(p j) t -> p j t", j=PACK)
+            raw = keep.tile([P, 2, t1 - t0], F32, name=f"x_raw{a}_{u}_{t0}")
+            nc.sync.dma_start(out=raw[:], in_=rows[:, 2 * u : 2 * u + 2, t0:t1])
+            if not x_raw:
+                nc.sync.dma_start(offsets[:], offs)
+            x_raw.append(raw)
+        w_raw = []
+        for a, c0, c1 in W_LOADS:
+            rows = w[a * K_PASS : (a + 1) * K_PASS, :].rearrange("(p j) c -> p j c", j=PACK)
+            raw = keep.tile([P, PACK, c1 - c0], F32, name=f"w_raw{a}_{c0}")
+            nc.sync.dma_start(out=raw[:], in_=rows[:, :, c0:c1])
+            w_raw.append(raw)
 
-        for step in STEPS:
-            kind = step[0]
-            if kind == "cx":
-                a, u = step[1:]
-                for (a2, u2, t0, t1), raw in x_raw.items():
-                    if (a2, u2) == (a, u):
-                        for engine, s0, s1 in X_SPLIT[2 * a + u]:
-                            lo, hi = max(s0, t0), min(s1, t1)
-                            if lo < hi:
-                                src = raw[:, :, lo - t0 : hi - t0].rearrange("p e t -> p t e")
-                                rounded_copy(engine, pairs[a, u][:, lo:hi, :], src)
-            elif kind == "g":
-                a, u = step[1:]
-                parts = X_PARTS[a] if u == 1 else 1
+        pairs = {(a, u): keep.tile([P, T, 2], BF16, name=f"pairs{a}_{u}") for a in range(PASSES) for u in range(2)}
+        for (a, u, t0, t1), raw, shares in zip(X_LOADS, x_raw, X_SHARES):
+            for engine, s0, s1 in shares:
+                src = raw[:, :, s0:s1].rearrange("p e t -> p t e")
+                round_to_bf16(nc, engine, pairs[a, u][:, t0 + s0 : t0 + s1, :], src)
+
+        w_grouped = []
+        for (a, c0, c1), raw, cut in zip(W_LOADS, w_raw, W_SCALAR_COLUMNS):
+            grouped = keep.tile([P, c1 - c0, PACK], BF16, name=f"w_grouped{a}_{c0}", align_bytes=64)
+            for engine, s0, s1 in (("scalar", 0, cut), ("vector", cut, c1 - c0)):
+                if s0 < s1:
+                    dst = grouped[:, s0:s1, :].rearrange("p (c i) j -> p c j i", i=RUN)
+                    src = raw[:, :, s0:s1].rearrange("p j (c i) -> p c j i", i=RUN)
+                    round_to_bf16(nc, engine, dst, src)
+            w_grouped.append(grouped)
+
+        picked = [keep.tile([P, 2, S, 2], BF16, name=f"picked{a}") for a in range(PASSES)]
+        for a in range(PASSES):
+            for u, parts in enumerate((WHOLE_LIST, LIST_HALVES)):
                 window = pairs[a, u][:].rearrange("p t e -> p (t e)").bitcast(U32)
                 dense = picked[a][:, u, :, :].rearrange("p s e -> p (s e)").bitcast(U32)
-                for h in range(parts):
-                    s0, s1 = h * S // parts, (h + 1) * S // parts
-                    nc.vector.tensor_copy(out=dense[:, s0:s1], in_=window.indirect(offsets[:, s0 // 16 : s1 // 16]))
-            elif kind == "il":
-                a = step[1]
-                parts = X_PARTS[a]
-                words = picked[a][:].rearrange("p u s e -> p (u s e)").bitcast(I32).rearrange("p (u s) -> p s u", u=2)
-                side_by_side = x_grouped[a][:].bitcast(I32).rearrange("p (s u) -> p s u", u=2)
-                for h in range(parts):
-                    s0, s1 = h * S // parts, (h + 1) * S // parts
-                    nc.vector.tensor_copy(out=side_by_side[:, s0:s1, :], in_=words[:, s0:s1, :])
-            elif kind == "qx":
-                a = step[1]
-                parts = X_PARTS[a]
-                for h in range(parts):
-                    s0, s1 = h * S // parts, (h + 1) * S // parts
-                    nc.vector.quantize_mx(
-                        out=x_codes[a][:, s0:s1].bitcast(FP8X4),
-                        scales=x_scales[a][:, s0:s1],
-                        in_=x_grouped[a][:, PACK * s0 : PACK * s1],
-                    )
-            elif kind == "cw":
-                i = step[1]
-                a, c0 = W_PIECES[i][:2]
-                for (a2, l0, l1), raw in w_raw.items():
-                    if a2 == a and l0 <= c0 < l1:
-                        for engine, s0, s1 in W_PIECES[i][3]:
-                            if s0 < s1:
-                                rounded_copy(
-                                    engine,
-                                    w_grouped[i][:, s0:s1, :].rearrange("p (c i) j -> p c j i", i=4),
-                                    raw[:, :, c0 - l0 + s0 : c0 - l0 + s1].rearrange("p j (c i) -> p c j i", i=4),
-                                )
-            elif kind == "qw":
-                i = step[1]
+                for part in parts:
+                    part_offsets = offsets[:, part.start // STRIPE : part.stop // STRIPE]
+                    nc.vector.tensor_copy(out=dense[:, part], in_=window.indirect(part_offsets))
+
+        x_codes = [keep.tile([P, S], U32, name=f"x_codes{a}", align_bytes=64) for a in range(PASSES)]
+        x_scales = [keep.tile([P, S], U8, name=f"x_scales{a}", align_bytes=64) for a in range(PASSES)]
+
+        def quantise_picked(a):
+            grouped = keep.tile([P, S * PACK], BF16, name=f"x_grouped{a}", align_bytes=64)
+            words = picked[a][:].rearrange("p u s e -> p (u s e)").bitcast(I32).rearrange("p (u s) -> p s u", u=2)
+            side_by_side = grouped[:].bitcast(I32).rearrange("p (s u) -> p s u", u=2)
+            for half in LIST_HALVES:
+                nc.vector.tensor_copy(out=side_by_side[:, half, :], in_=words[:, half, :])
+            for half in LIST_HALVES:
                 nc.vector.quantize_mx(
-                    out=w_codes[i][:].bitcast(FP8X4),
-                    scales=w_scales[i][:],
-                    in_=w_grouped[i][:].rearrange("p c j -> p (c j)"),
+                    out=x_codes[a][:, half].bitcast(FP8X4),
+                    scales=x_scales[a][:, half],
+                    in_=grouped[:, PACK * half.start : PACK * half.stop],
                 )
-            elif kind == "wm":
-                source, i = WARM[step[1]]
-                a = i if source == "qx" else 0
-                codes, scales = (x_codes[i], x_scales[i]) if source == "qx" else (w_codes[i], w_scales[i])
-                nc.tensor.matmul_mx(
-                    out=spare[:],
-                    lhsT=codes[:, 0:P].bitcast(FP8X4),
-                    lhsT_scale=scales[:, 0:P],
-                    rhs=x_codes[a][:].bitcast(FP8X4),
-                    rhs_scale=x_scales[a][:],
-                    start=True,
-                    stop=True,
+
+        for a in range(PASSES - 1):
+            quantise_picked(a)
+
+        spare_bank = psum.tile([P, S], F32, name="spare_bank")
+        warm_codes, warm_scales = x_codes[PASSES - 2], x_scales[PASSES - 2]
+        for r in range(WARM_UP_PASSES):
+            nc.tensor.matmul_mx(
+                out=spare_bank[:],
+                lhsT=warm_codes[:, 0:P].bitcast(FP8X4),
+                lhsT_scale=warm_scales[:, 0:P],
+                rhs=warm_codes[:].bitcast(FP8X4),
+                rhs_scale=warm_scales[:],
+                start=True,
+                stop=True,
+            )
+
+        w_codes, w_scales = [], []
+        for (a, c0, c1), grouped in zip(W_LOADS, w_grouped):
+            codes = keep.tile([P, c1 - c0], U32, name=f"w_codes{a}_{c0}", align_bytes=64)
+            scales = keep.tile([P, c1 - c0], U8, name=f"w_scales{a}_{c0}", align_bytes=64)
+            nc.vector.quantize_mx(
+                out=codes[:].bitcast(FP8X4), scales=scales[:], in_=grouped[:].rearrange("p c j -> p (c j)")
+            )
+            w_codes.append(codes)
+            w_scales.append(scales)
+
+        quantise_picked(PASSES - 1)
+
+        sums = [
+            [psum.tile([P, g.stop - g.start], F32, name=f"sums{m}_{g.start}") for g in PSUM_GROUPS[m]]
+            for m in range(M_TILES)
+        ]
+        for (a, c0, c1), codes, scales in zip(W_LOADS, w_codes, w_scales):
+            for m in range(c0 // P, c1 // P):
+                columns = slice(m * P - c0, (m + 1) * P - c0)
+                for group, bank in zip(PSUM_GROUPS[m], sums[m]):
+                    nc.tensor.matmul_mx(
+                        out=bank[:],
+                        lhsT=codes[:, columns].bitcast(FP8X4),
+                        lhsT_scale=scales[:, columns],
+                        rhs=x_codes[a][:, group].bitcast(FP8X4),
+                        rhs_scale=x_scales[a][:, group],
+                        start=(a == 0),
+                        stop=(a == PASSES - 1),
+                    )
+
+        activated = {}
+        for m in range(M_TILES):
+            for group, bank in zip(PSUM_GROUPS[m], sums[m]):
+                for part in EPILOGUE_PARTS[m]:
+                    if group.start <= part.start < group.stop:
+                        y = keep.tile([P, part.stop - part.start], F32, name=f"y{m}_{part.start}")
+                        src = bank[:, part.start - group.start : part.stop - group.start]
+                        nc.scalar.activation(out=y[:], in_=src, func=GELU, bias=bias[:, m : m + 1])
+                        activated[m, part.start] = y
+
+        for m in range(M_TILES):
+            pooled = keep.tile([P, V], F32, name=f"pooled{m}")
+            for part in EPILOGUE_PARTS[m]:
+                nc.vector.tensor_reduce(
+                    out=pooled[:, part.start // D : part.stop // D],
+                    in_=activated[m, part.start][:].rearrange("p (v d) -> p v d", d=D),
+                    axis=mybir.AxisListType.X,
+                    op=mybir.AluOpType.max,
                 )
-            elif kind == "mm":
-                i = step[1]
-                a, c0, c1 = W_PIECES[i][:3]
-                for m in range(c0 // P, c1 // P):
-                    cols = slice(m * P - c0, (m + 1) * P - c0)
-                    for h in range(N_SPLIT[m]):
-                        picks = slice(h * S // N_SPLIT[m], (h + 1) * S // N_SPLIT[m])
-                        nc.tensor.matmul_mx(
-                            out=acc[m, h][:],
-                            lhsT=w_codes[i][:, cols].bitcast(FP8X4),
-                            lhsT_scale=w_scales[i][:, cols],
-                            rhs=x_codes[a][:, picks].bitcast(FP8X4),
-                            rhs_scale=x_scales[a][:, picks],
-                            start=(passes_done[m] == 0),
-                            stop=(passes_done[m] == PASSES - 1),
-                        )
-                    passes_done[m] += 1
-            elif kind == "gelu":
-                m = step[1]
-                parts = TAIL_PARTS[m]
-                width = S // parts
-                for h in range(parts):
-                    g, n0 = divmod(h * width, S // N_SPLIT[m])
-                    y[m, h] = keep.tile([P, width], F32, name=f"y{m}_{h}")
-                    nc.scalar.activation(
-                        out=y[m, h][:], in_=acc[m, g][:, n0 : n0 + width], func=GELU, bias=bias[:, m : m + 1]
-                    )
-            else:
-                m = step[1]
-                parts = TAIL_PARTS[m]
-                for h in range(parts):
-                    nc.vector.tensor_reduce(
-                        out=pooled[m][:, h * V // parts : (h + 1) * V // parts],
-                        in_=y[m, h][:].rearrange("p (v d) -> p v d", d=D),
-                        axis=mybir.AxisListType.X,
-                        op=mybir.AluOpType.max,
-                    )
-                nc.sync.dma_start(out=out[m * P : (m + 1) * P, :], in_=pooled[m][:])
+            nc.sync.dma_start(out=out[m * P : (m + 1) * P, :], in_=pooled[:])

@@ -71,10 +71,6 @@ def tile_picked_pool_lin_gelu_sub_e_kernel(tc, xT, w, b, offs, out):
         keep = ctx.enter_context(tc.tile_pool(name="keep", bufs=1))
         psum = ctx.enter_context(tc.psum_pool(name="psum", bufs=1))
 
-        bias_rows = keep.tile([P, P], F32, name="bias_rows")
-        nc.gpsimd.memset(bias_rows[:], 0.0)
-        nc.scalar.dma_start(out=bias_rows[0:M_TILES, :], in_=b.rearrange("(m p) o -> m (p o)", p=P))
-
         zeros = keep.tile([P, 8], F32, name="zeros")
         nc.gpsimd.memset(zeros[:], 0.0)
         gelu_of_zeros = keep.tile([P, 8], F32, name="gelu_of_zeros")
@@ -82,10 +78,8 @@ def tile_picked_pool_lin_gelu_sub_e_kernel(tc, xT, w, b, offs, out):
 
         identity = keep.tile([P, P], F32, name="identity")
         make_identity(nc, identity[:])
-        bias_bank = psum.tile([P, P], F32, name="bias_bank")
-        nc.tensor.transpose(bias_bank[:], bias_rows[:], identity[:])
-        bias = keep.tile([P, M_TILES], F32, name="bias")
-        nc.vector.tensor_copy(out=bias[:], in_=bias_bank[:, 0:M_TILES])
+        bias_rows = keep.tile([P, P], F32, name="bias_rows")
+        nc.gpsimd.memset(bias_rows[:], 0.0)
 
         offsets = keep.tile([P, S // STRIPE], U16, name="offsets")
         x_raw = []
@@ -93,15 +87,22 @@ def tile_picked_pool_lin_gelu_sub_e_kernel(tc, xT, w, b, offs, out):
             rows = xT[a * K_PASS : (a + 1) * K_PASS, :].rearrange("(p j) t -> p j t", j=PACK)
             raw = keep.tile([P, 2, t1 - t0], F32, name=f"x_raw{a}_{u}_{t0}")
             nc.sync.dma_start(out=raw[:], in_=rows[:, 2 * u : 2 * u + 2, t0:t1])
-            if not x_raw:
-                nc.sync.dma_start(offsets[:], offs)
             x_raw.append(raw)
+            if len(x_raw) == 1:
+                nc.sync.dma_start(offsets[:], offs)
+            if len(x_raw) == 2:
+                nc.sync.dma_start(out=bias_rows[0:M_TILES, :], in_=b.rearrange("(m p) o -> m (p o)", p=P))
         w_raw = []
         for a, c0, c1 in W_LOADS:
             rows = w[a * K_PASS : (a + 1) * K_PASS, :].rearrange("(p j) c -> p j c", j=PACK)
             raw = keep.tile([P, PACK, c1 - c0], F32, name=f"w_raw{a}_{c0}")
             nc.sync.dma_start(out=raw[:], in_=rows[:, :, c0:c1])
             w_raw.append(raw)
+
+        bias_bank = psum.tile([P, P], F32, name="bias_bank")
+        nc.tensor.transpose(bias_bank[:], bias_rows[:], identity[:])
+        bias = keep.tile([P, M_TILES], F32, name="bias")
+        nc.vector.tensor_copy(out=bias[:], in_=bias_bank[:, 0:M_TILES])
 
         pairs = {(a, u): keep.tile([P, T, 2], BF16, name=f"pairs{a}_{u}") for a in range(PASSES) for u in range(2)}
         for (a, u, t0, t1), raw, shares in zip(X_LOADS, x_raw, X_SHARES):

@@ -26,36 +26,19 @@ RUN = 4
 
 X_LOADS = [(0, 0, 0, T), (0, 1, 0, T), (1, 0, 0, T), (1, 1, 0, T), (2, 0, 0, T), (2, 1, 0, T // 2), (2, 1, T // 2, T)]
 
-X_SHARES = [
-    [("scalar", 0, 320), ("vector", 320, 1024)],
-    [("vector", 0, 640), ("scalar", 640, 1024)],
-    [("scalar", 0, 768), ("vector", 768, 1024)],
-    [("vector", 0, 384), ("scalar", 384, 1024)],
-    [("scalar", 0, 704), ("vector", 704, 1024)],
-    [("scalar", 0, 512)],
-    [("scalar", 0, 512)],
-]
+X_SHARES = [[("scalar", 0, s), ("vector", s, t1 - t0)] if s < t1 - t0 else [("scalar", 0, s)] for s, (a, u, t0, t1) in zip([352, 352, 704, 704, 704, 512, 512], X_LOADS)]
 
-W_LOADS = [
-    (0, 0, 256),
-    (1, 0, 256),
-    (2, 0, 256),
-    (0, 256, 512),
-    (1, 256, 384),
-    (2, 256, 384),
-    (1, 384, 512),
-    (2, 384, 512),
-]
+W_LOADS = [(0, 0, 256), (1, 0, 256), (2, 0, 256), (0, 256, 512), (1, 256, 384), (2, 256, 384), (1, 384, 512), (2, 384, 512)]
 
-W_SCALAR_COLUMNS = [96, 256, 256, 256, 64, 128, 96, 0]
+W_SCALAR_COLUMNS = [88, 256, 256, 256, 64, 128, 64, 0]
 
 LIST_HALVES = [slice(0, S // 2), slice(S // 2, S)]
 WHOLE_LIST = [slice(0, S)]
 
-PSUM_GROUPS = [WHOLE_LIST, WHOLE_LIST, WHOLE_LIST, LIST_HALVES]
-EPILOGUE_PARTS = [WHOLE_LIST, WHOLE_LIST, LIST_HALVES, LIST_HALVES]
+PSUM_GROUPS = [LIST_HALVES] * M_TILES
+EPILOGUE_PARTS = PSUM_GROUPS
 
-WARM_UP_PASSES = 3
+WARM_UP_PASSES = 2
 
 
 def round_to_bf16(nc, engine, dst, src):
@@ -85,7 +68,7 @@ def tile_picked_pool_lin_gelu_sub_e_kernel(tc, xT, w, b, offs, out):
         x_raw = []
         for a, u, t0, t1 in X_LOADS:
             rows = xT[a * K_PASS : (a + 1) * K_PASS, :].rearrange("(p j) t -> p j t", j=PACK)
-            raw = keep.tile([P, 2, t1 - t0], F32, name=f"x_raw{a}_{u}_{t0}")
+            raw = keep.tile([P, 2, t1 - t0], F32, name=f"x_raw{a}_{u}_{t0}", tag=f"x_raw{a}_{u}_{t0}")
             nc.sync.dma_start(out=raw[:], in_=rows[:, 2 * u : 2 * u + 2, t0:t1])
             x_raw.append(raw)
             if len(x_raw) == 1:
@@ -99,16 +82,17 @@ def tile_picked_pool_lin_gelu_sub_e_kernel(tc, xT, w, b, offs, out):
             nc.sync.dma_start(out=raw[:], in_=rows[:, :, c0:c1])
             w_raw.append(raw)
 
-        bias_bank = psum.tile([P, P], F32, name="bias_bank")
+        bias_bank = psum.tile([P, P], F32, name="bias_bank", tag="spare")
         nc.tensor.transpose(bias_bank[:], bias_rows[:], identity[:])
-        bias = keep.tile([P, M_TILES], F32, name="bias")
-        nc.vector.tensor_copy(out=bias[:], in_=bias_bank[:, 0:M_TILES])
 
         pairs = {(a, u): keep.tile([P, T, 2], BF16, name=f"pairs{a}_{u}") for a in range(PASSES) for u in range(2)}
         for (a, u, t0, t1), raw, shares in zip(X_LOADS, x_raw, X_SHARES):
             for engine, s0, s1 in shares:
                 src = raw[:, :, s0:s1].rearrange("p e t -> p t e")
                 round_to_bf16(nc, engine, pairs[a, u][:, t0 + s0 : t0 + s1, :], src)
+
+        bias = keep.tile([P, M_TILES], F32, name="bias", tag=f"x_raw{PASSES - 1}_1_{T // 2}")
+        nc.vector.tensor_copy(out=bias[:], in_=bias_bank[:, 0:M_TILES])
 
         w_grouped = []
         for (a, c0, c1), raw, cut in zip(W_LOADS, w_raw, W_SCALAR_COLUMNS):
@@ -148,7 +132,7 @@ def tile_picked_pool_lin_gelu_sub_e_kernel(tc, xT, w, b, offs, out):
         for a in range(PASSES - 1):
             quantise_picked(a)
 
-        spare_bank = psum.tile([P, S], F32, name="spare_bank")
+        spare_bank = psum.tile([P, S], F32, name="spare_bank", tag="spare")
         warm_codes, warm_scales = x_codes[PASSES - 2], x_scales[PASSES - 2]
         for r in range(WARM_UP_PASSES):
             nc.tensor.matmul_mx(
@@ -174,7 +158,7 @@ def tile_picked_pool_lin_gelu_sub_e_kernel(tc, xT, w, b, offs, out):
         quantise_picked(PASSES - 1)
 
         sums = [
-            [psum.tile([P, g.stop - g.start], F32, name=f"sums{m}_{g.start}") for g in PSUM_GROUPS[m]]
+            [psum.tile([P, g.stop - g.start], F32, name=f"sums{m}_{g.start}", tag="spare" if (m, g.stop) == (M_TILES - 1, S) else f"sums{m}_{g.start}") for g in PSUM_GROUPS[m]]
             for m in range(M_TILES)
         ]
         for (a, c0, c1), codes, scales in zip(W_LOADS, w_codes, w_scales):

@@ -38,8 +38,6 @@ WHOLE_LIST = [slice(0, S)]
 PSUM_GROUPS = [LIST_HALVES] * M_TILES
 EPILOGUE_PARTS = PSUM_GROUPS
 
-WARM_UP_PASSES = 2
-
 
 def round_to_bf16(nc, engine, dst, src):
     if engine == "scalar":
@@ -131,19 +129,6 @@ def tile_picked_pool_lin_gelu_sub_e_kernel(tc, xT, w, b, offs, out):
 
         for a in range(PASSES - 1):
             quantise_picked(a)
-
-        spare_bank = psum.tile([P, S], F32, name="spare_bank", tag="spare")
-        warm_codes, warm_scales = x_codes[PASSES - 2], x_scales[PASSES - 2]
-        for r in range(WARM_UP_PASSES):
-            nc.tensor.matmul_mx(
-                out=spare_bank[:],
-                lhsT=warm_codes[:, 0:P].bitcast(FP8X4),
-                lhsT_scale=warm_scales[:, 0:P],
-                rhs=warm_codes[:].bitcast(FP8X4),
-                rhs_scale=warm_scales[:],
-                start=True,
-                stop=True,
-            )
 
         w_codes, w_scales = [], []
         for (a, c0, c1), grouped in zip(W_LOADS, w_grouped):

@@ -24,19 +24,14 @@ M_TILES = N // P
 STRIPE = 16
 RUN = 4
 
-X_LOADS = [(0, 0, 0, T), (0, 1, 0, T), (1, 0, 0, T), (1, 1, 0, T), (2, 0, 0, T), (2, 1, 0, T // 2), (2, 1, T // 2, T)]
-
-X_SHARES = [[("scalar", 0, s), ("vector", s, t1 - t0)] if s < t1 - t0 else [("scalar", 0, s)] for s, (a, u, t0, t1) in zip([352, 352, 704, 704, 704, 512, 512], X_LOADS)]
-
+X_LOADS = [(0, 0, 0, 1024, 352), (0, 1, 0, 1024, 352), (1, 0, 0, 1024, 704), (1, 1, 0, 512, 512), (1, 1, 512, 1024, 352), (2, 0, 0, 512, 512), (2, 0, 512, 1024, 512), (2, 1, 0, 512, 512), (2, 1, 512, 1024, 512)]
 W_LOADS = [(0, 0, 256), (1, 0, 256), (2, 0, 256), (0, 256, 512), (1, 256, 384), (2, 256, 384), (1, 384, 512), (2, 384, 512)]
-
-W_SCALAR_COLUMNS = [88, 256, 256, 256, 64, 128, 64, 0]
-
-LIST_HALVES = [slice(0, S // 2), slice(S // 2, S)]
-WHOLE_LIST = [slice(0, S)]
-
-PSUM_GROUPS = [LIST_HALVES] * M_TILES
-EPILOGUE_PARTS = PSUM_GROUPS
+W_PIECES = [(0, 0, 128, 0), (0, 128, 256, 0), (1, 0, 256, 256), (2, 0, 256, 256), (3, 256, 512, 192), (4, 256, 384, 0), (5, 256, 384, 128), (6, 384, 512, 64), (7, 384, 512, 0)]
+HALVES = [slice(0, S // 2), slice(S // 2, S)]
+WHOLE = [slice(0, S)]
+TAGS = {"bias": "x_raw8", "y01": "w_raw5"}
+PARTS = [HALVES] * M_TILES
+GROUPS = [HALVES] * M_TILES
 
 
 def round_to_bf16(nc, engine, dst, src):
@@ -52,131 +47,178 @@ def tile_picked_pool_lin_gelu_sub_e_kernel(tc, xT, w, b, offs, out):
         keep = ctx.enter_context(tc.tile_pool(name="keep", bufs=1))
         psum = ctx.enter_context(tc.psum_pool(name="psum", bufs=1))
 
-        zeros = keep.tile([P, 8], F32, name="zeros")
+        def sb(shape, dtype, name):
+            return keep.tile(shape, dtype, name=name, tag=TAGS.get(name, name), align_bytes=64)
+
+        zeros = sb([P, 8], F32, "zeros")
         nc.gpsimd.memset(zeros[:], 0.0)
-        gelu_of_zeros = keep.tile([P, 8], F32, name="gelu_of_zeros")
+        gelu_of_zeros = sb([P, 8], F32, "gelu_of_zeros")
         nc.scalar.activation(out=gelu_of_zeros[:], in_=zeros[:], func=GELU)
 
-        identity = keep.tile([P, P], F32, name="identity")
+        identity = sb([P, P], F32, "identity")
         make_identity(nc, identity[:])
-        bias_rows = keep.tile([P, P], F32, name="bias_rows")
+        bias_rows = sb([P, P], F32, "bias_rows")
         nc.gpsimd.memset(bias_rows[:], 0.0)
 
         offsets = keep.tile([P, S // STRIPE], U16, name="offsets")
         x_raw = []
-        for a, u, t0, t1 in X_LOADS:
+        for i, (a, u, t0, t1, cut) in enumerate(X_LOADS):
             rows = xT[a * K_PASS : (a + 1) * K_PASS, :].rearrange("(p j) t -> p j t", j=PACK)
-            raw = keep.tile([P, 2, t1 - t0], F32, name=f"x_raw{a}_{u}_{t0}", tag=f"x_raw{a}_{u}_{t0}")
+            raw = sb([P, 2, t1 - t0], F32, f"x_raw{i}")
             nc.sync.dma_start(out=raw[:], in_=rows[:, 2 * u : 2 * u + 2, t0:t1])
             x_raw.append(raw)
-            if len(x_raw) == 1:
+            if i == 0:
                 nc.sync.dma_start(offsets[:], offs)
-            if len(x_raw) == 2:
+            if i == 1:
                 nc.sync.dma_start(out=bias_rows[0:M_TILES, :], in_=b.rearrange("(m p) o -> m (p o)", p=P))
         w_raw = []
-        for a, c0, c1 in W_LOADS:
+        for i, (a, c0, c1) in enumerate(W_LOADS):
             rows = w[a * K_PASS : (a + 1) * K_PASS, :].rearrange("(p j) c -> p j c", j=PACK)
-            raw = keep.tile([P, PACK, c1 - c0], F32, name=f"w_raw{a}_{c0}")
+            raw = sb([P, PACK, c1 - c0], F32, f"w_raw{i}")
             nc.sync.dma_start(out=raw[:], in_=rows[:, :, c0:c1])
             w_raw.append(raw)
 
         bias_bank = psum.tile([P, P], F32, name="bias_bank", tag="spare")
         nc.tensor.transpose(bias_bank[:], bias_rows[:], identity[:])
 
-        pairs = {(a, u): keep.tile([P, T, 2], BF16, name=f"pairs{a}_{u}") for a in range(PASSES) for u in range(2)}
-        for (a, u, t0, t1), raw, shares in zip(X_LOADS, x_raw, X_SHARES):
-            for engine, s0, s1 in shares:
-                src = raw[:, :, s0:s1].rearrange("p e t -> p t e")
-                round_to_bf16(nc, engine, pairs[a, u][:, t0 + s0 : t0 + s1, :], src)
+        pairs = {(a, u): sb([P, T, 2], BF16, f"pairs{a}_{u}") for a in range(PASSES) for u in range(2)}
+        picked = [sb([P, 2, S, 2], BF16, f"picked{a}") for a in range(PASSES)]
+        x_codes = [sb([P, S], U32, f"x_codes{a}") for a in range(PASSES)]
+        x_scales = [sb([P, S], U8, f"x_scales{a}") for a in range(PASSES)]
+        x_grouped, w_grouped, w_codes, w_scales, sums, activated, pooled, held = {}, {}, {}, {}, {}, {}, {}, {}
 
-        bias = keep.tile([P, M_TILES], F32, name="bias", tag=f"x_raw{PASSES - 1}_1_{T // 2}")
-        nc.vector.tensor_copy(out=bias[:], in_=bias_bank[:, 0:M_TILES])
+        def round_x(i):
+            a, u, t0, t1, cut = X_LOADS[i]
+            for engine, s0, s1 in (("scalar", 0, cut), ("vector", cut, t1 - t0)):
+                if s0 < s1:
+                    src = x_raw[i][:, :, s0:s1].rearrange("p e t -> p t e")
+                    round_to_bf16(nc, engine, pairs[a, u][:, t0 + s0 : t0 + s1, :], src)
 
-        w_grouped = []
-        for (a, c0, c1), raw, cut in zip(W_LOADS, w_raw, W_SCALAR_COLUMNS):
-            grouped = keep.tile([P, c1 - c0, PACK], BF16, name=f"w_grouped{a}_{c0}", align_bytes=64)
+        def gather(a, u, parts):
+            window = pairs[a, u][:].rearrange("p t e -> p (t e)").bitcast(U32)
+            dense = picked[a][:, u, :, :].rearrange("p s e -> p (s e)").bitcast(U32)
+            for part in parts:
+                part_offsets = offsets[:, part.start // STRIPE : part.stop // STRIPE]
+                nc.vector.tensor_copy(out=dense[:, part], in_=window.indirect(part_offsets))
+
+        def weave(a, parts, engine="vector"):
+            if a not in x_grouped:
+                x_grouped[a] = sb([P, S * PACK], BF16, f"x_grouped{a}")
+            dt = I32 if engine == "vector" else U32
+            words = picked[a][:].rearrange("p u s e -> p (u s e)").bitcast(dt).rearrange("p (u s) -> p s u", u=2)
+            side_by_side = x_grouped[a][:].bitcast(dt).rearrange("p (s u) -> p s u", u=2)
+            for part in parts:
+                if engine == "vector":
+                    nc.vector.tensor_copy(out=side_by_side[:, part, :], in_=words[:, part, :])
+                else:
+                    nc.scalar.copy(out=side_by_side[:, part, :], in_=words[:, part, :])
+
+        def quantise_x(a, parts):
+            for part in parts:
+                nc.vector.quantize_mx(
+                    out=x_codes[a][:, part].bitcast(FP8X4),
+                    scales=x_scales[a][:, part],
+                    in_=x_grouped[a][:, PACK * part.start : PACK * part.stop],
+                )
+
+        def round_w(i):
+            load, c0, c1, cut = W_PIECES[i]
+            first = c0 - W_LOADS[load][1]
+            grouped = sb([P, c1 - c0, PACK], BF16, f"w_grouped{i}")
             for engine, s0, s1 in (("scalar", 0, cut), ("vector", cut, c1 - c0)):
                 if s0 < s1:
                     dst = grouped[:, s0:s1, :].rearrange("p (c i) j -> p c j i", i=RUN)
-                    src = raw[:, :, s0:s1].rearrange("p j (c i) -> p c j i", i=RUN)
+                    src = w_raw[load][:, :, first + s0 : first + s1].rearrange("p j (c i) -> p c j i", i=RUN)
                     round_to_bf16(nc, engine, dst, src)
-            w_grouped.append(grouped)
+            w_grouped[i] = grouped
 
-        picked = [keep.tile([P, 2, S, 2], BF16, name=f"picked{a}") for a in range(PASSES)]
-        for a in range(PASSES):
-            for u, parts in enumerate((WHOLE_LIST, LIST_HALVES)):
-                window = pairs[a, u][:].rearrange("p t e -> p (t e)").bitcast(U32)
-                dense = picked[a][:, u, :, :].rearrange("p s e -> p (s e)").bitcast(U32)
-                for part in parts:
-                    part_offsets = offsets[:, part.start // STRIPE : part.stop // STRIPE]
-                    nc.vector.tensor_copy(out=dense[:, part], in_=window.indirect(part_offsets))
-
-        x_codes = [keep.tile([P, S], U32, name=f"x_codes{a}", align_bytes=64) for a in range(PASSES)]
-        x_scales = [keep.tile([P, S], U8, name=f"x_scales{a}", align_bytes=64) for a in range(PASSES)]
-
-        def quantise_picked(a):
-            grouped = keep.tile([P, S * PACK], BF16, name=f"x_grouped{a}", align_bytes=64)
-            words = picked[a][:].rearrange("p u s e -> p (u s e)").bitcast(I32).rearrange("p (u s) -> p s u", u=2)
-            side_by_side = grouped[:].bitcast(I32).rearrange("p (s u) -> p s u", u=2)
-            for half in LIST_HALVES:
-                nc.vector.tensor_copy(out=side_by_side[:, half, :], in_=words[:, half, :])
-            for half in LIST_HALVES:
-                nc.vector.quantize_mx(
-                    out=x_codes[a][:, half].bitcast(FP8X4),
-                    scales=x_scales[a][:, half],
-                    in_=grouped[:, PACK * half.start : PACK * half.stop],
-                )
-
-        for a in range(PASSES - 1):
-            quantise_picked(a)
-
-        w_codes, w_scales = [], []
-        for (a, c0, c1), grouped in zip(W_LOADS, w_grouped):
-            codes = keep.tile([P, c1 - c0], U32, name=f"w_codes{a}_{c0}", align_bytes=64)
-            scales = keep.tile([P, c1 - c0], U8, name=f"w_scales{a}_{c0}", align_bytes=64)
+        def quantise_w(i):
+            load, c0, c1, cut = W_PIECES[i]
+            w_codes[i] = sb([P, c1 - c0], U32, f"w_codes{i}")
+            w_scales[i] = sb([P, c1 - c0], U8, f"w_scales{i}")
             nc.vector.quantize_mx(
-                out=codes[:].bitcast(FP8X4), scales=scales[:], in_=grouped[:].rearrange("p c j -> p (c j)")
+                out=w_codes[i][:].bitcast(FP8X4), scales=w_scales[i][:], in_=w_grouped[i][:].rearrange("p c j -> p (c j)")
             )
-            w_codes.append(codes)
-            w_scales.append(scales)
 
-        quantise_picked(PASSES - 1)
-
-        sums = [
-            [psum.tile([P, g.stop - g.start], F32, name=f"sums{m}_{g.start}", tag="spare" if (m, g.stop) == (M_TILES - 1, S) else f"sums{m}_{g.start}") for g in PSUM_GROUPS[m]]
-            for m in range(M_TILES)
-        ]
-        for (a, c0, c1), codes, scales in zip(W_LOADS, w_codes, w_scales):
-            for m in range(c0 // P, c1 // P):
+        def multiply(i, tiles=None):
+            load, c0, c1, cut = W_PIECES[i]
+            a = W_LOADS[load][0]
+            for m in tiles or range(c0 // P, c1 // P):
                 columns = slice(m * P - c0, (m + 1) * P - c0)
-                for group, bank in zip(PSUM_GROUPS[m], sums[m]):
+                for g in GROUPS[m]:
+                    if a == 0:
+                        last = (m, g.stop) == (M_TILES - 1, S)
+                        sums[m, g.start] = psum.tile([P, g.stop - g.start], F32, name=f"sums{m}_{g.start}", tag="spare" if last else f"sums{m}_{g.start}")
                     nc.tensor.matmul_mx(
-                        out=bank[:],
-                        lhsT=codes[:, columns].bitcast(FP8X4),
-                        lhsT_scale=scales[:, columns],
-                        rhs=x_codes[a][:, group].bitcast(FP8X4),
-                        rhs_scale=x_scales[a][:, group],
+                        out=sums[m, g.start][:],
+                        lhsT=w_codes[i][:, columns].bitcast(FP8X4),
+                        lhsT_scale=w_scales[i][:, columns],
+                        rhs=x_codes[a][:, g].bitcast(FP8X4),
+                        rhs_scale=x_scales[a][:, g],
                         start=(a == 0),
                         stop=(a == PASSES - 1),
                     )
 
-        activated = {}
-        for m in range(M_TILES):
-            for group, bank in zip(PSUM_GROUPS[m], sums[m]):
-                for part in EPILOGUE_PARTS[m]:
-                    if group.start <= part.start < group.stop:
-                        y = keep.tile([P, part.stop - part.start], F32, name=f"y{m}_{part.start}")
-                        src = bank[:, part.start - group.start : part.stop - group.start]
-                        nc.scalar.activation(out=y[:], in_=src, func=GELU, bias=bias[:, m : m + 1])
-                        activated[m, part.start] = y
+        def take_bias():
+            held["bias"] = sb([P, M_TILES], F32, "bias")
+            nc.vector.tensor_copy(out=held["bias"][:], in_=bias_bank[:, 0:M_TILES])
 
-        for m in range(M_TILES):
-            pooled = keep.tile([P, V], F32, name=f"pooled{m}")
-            for part in EPILOGUE_PARTS[m]:
+        def activate(m, parts=HALVES):
+            if m not in activated:
+                if m < 2:
+                    if "y01" not in held:
+                        held["y01"] = sb([P, 2, S], F32, "y01")
+                    activated[m] = held["y01"][:, m, :]
+                else:
+                    activated[m] = sb([P, S], F32, f"y{m}")[:]
+            for part in parts:
+                g = [g for g in GROUPS[m] if g.start <= part.start < g.stop][0]
+                src = sums[m, g.start][:, part.start - g.start : part.stop - g.start]
+                nc.scalar.activation(out=activated[m][:, part], in_=src, func=GELU, bias=held["bias"][:, m : m + 1])
+
+        def pool(m, parts=HALVES):
+            if m not in pooled:
+                pooled[m] = sb([P, V], F32, f"pooled{m}")
+            for part in parts:
                 nc.vector.tensor_reduce(
-                    out=pooled[:, part.start // D : part.stop // D],
-                    in_=activated[m, part.start][:].rearrange("p (v d) -> p v d", d=D),
+                    out=pooled[m][:, part.start // D : part.stop // D],
+                    in_=activated[m][:, part].rearrange("p (v d) -> p v d", d=D),
                     axis=mybir.AxisListType.X,
                     op=mybir.AluOpType.max,
                 )
-            nc.sync.dma_start(out=out[m * P : (m + 1) * P, :], in_=pooled[:])
+
+        def store(m):
+            nc.sync.dma_start(out=out[m * P : (m + 1) * P, :], in_=pooled[m][:])
+
+        def clock(name, src):
+            tick = keep.tile([P, 1], src.dtype, name=name)
+            nc.gpsimd.tensor_copy(out=tick[:], in_=src)
+
+        A, B = HALVES[:1], HALVES[1:]
+        for i in range(len(X_LOADS)):
+            round_x(i)
+        take_bias()
+        for i in range(len(W_PIECES)):
+            round_w(i)
+        quantise_w(0)
+        for a in range(PASSES - 1):
+            gather(a, 0, WHOLE)
+            gather(a, 1, HALVES)
+        gather(2, 0, WHOLE)
+        gather(2, 1, A)
+        for a in range(PASSES - 1):
+            weave(a, HALVES)
+            quantise_x(a, HALVES)
+        quantise_w(1)
+        gather(2, 1, B)
+        for i in range(2, len(W_PIECES)):
+            quantise_w(i)
+        weave(2, HALVES)
+        quantise_x(2, HALVES)
+        for i in range(len(W_PIECES)):
+            multiply(i)
+        for m in range(M_TILES):
+            activate(m)
+        for m in range(M_TILES):
+            pool(m)
+            store(m)

@@ -48,7 +48,7 @@ def tile_picked_pool_lin_gelu_sub_e_kernel(tc, xT, w, b, offs, out):
         psum = ctx.enter_context(tc.psum_pool(name="psum", bufs=1))
 
         def sb(shape, dtype, name):
-            return keep.tile(shape, dtype, name=name, tag=TAGS.get(name, name), align_bytes=64)
+            return keep.tile(shape, dtype, name=name, tag=TAGS.get(name, name), align_bytes=256)
 
         zeros = sb([P, 8], F32, "zeros")
         nc.gpsimd.memset(zeros[:], 0.0)

@@ -23,15 +23,12 @@ PASSES = K // K_PASS
 M_TILES = N // P
 STRIPE = 16
 RUN = 4
+HALF = S // 2
 
-X_LOADS = [(0, 0, 0, 1024, 352), (0, 1, 0, 1024, 352), (1, 0, 0, 1024, 704), (1, 1, 0, 512, 512), (1, 1, 512, 1024, 352), (2, 0, 0, 512, 512), (2, 0, 512, 1024, 512), (2, 1, 0, 512, 512), (2, 1, 512, 1024, 512)]
+X_LOADS = [(0, 0, 0, 1024, 352), (0, 1, 0, 1024, 352), (1, 0, 0, 1024, 512), (1, 1, 0, 512, 512), (1, 1, 512, 1024, 512), (2, 0, 0, 512, 512), (2, 0, 512, 1024, 512), (2, 1, 0, 512, 512), (2, 1, 512, 1024, 320)]
 W_LOADS = [(0, 0, 256), (1, 0, 256), (2, 0, 256), (0, 256, 512), (1, 256, 384), (2, 256, 384), (1, 384, 512), (2, 384, 512)]
-W_PIECES = [(0, 0, 128, 0), (0, 128, 256, 0), (1, 0, 256, 256), (2, 0, 256, 256), (3, 256, 512, 192), (4, 256, 384, 0), (5, 256, 384, 128), (6, 384, 512, 64), (7, 384, 512, 0)]
-HALVES = [slice(0, S // 2), slice(S // 2, S)]
-WHOLE = [slice(0, S)]
-TAGS = {"bias": "x_raw8", "y01": "w_raw5"}
-PARTS = [HALVES] * M_TILES
-GROUPS = [HALVES] * M_TILES
+W_PIECES = {"A": (0, 0, 256, 256), "B0": (1, 0, 128, 128), "B1": (1, 128, 256, 128), "C0": (2, 0, 128, 128), "C1": (2, 128, 256, 128), "D": (3, 256, 512, 128), "E": (4, 256, 384, 128), "F": (5, 256, 384, 0), "G": (6, 384, 512, 128), "H": (7, 384, 512, 0)}
+TAGS = {"x_grouped2": "w_raw0", "x_codes2_1": "w_raw1", "w_codesB1": "w_raw2", "y0": "w_raw3", "y1": "w_groupedF"}
 
 
 def round_to_bf16(nc, engine, dst, src):
@@ -83,9 +80,8 @@ def tile_picked_pool_lin_gelu_sub_e_kernel(tc, xT, w, b, offs, out):
 
         pairs = {(a, u): sb([P, T, 2], BF16, f"pairs{a}_{u}") for a in range(PASSES) for u in range(2)}
         picked = [sb([P, 2, S, 2], BF16, f"picked{a}") for a in range(PASSES)]
-        x_codes = [sb([P, S], U32, f"x_codes{a}") for a in range(PASSES)]
-        x_scales = [sb([P, S], U8, f"x_scales{a}") for a in range(PASSES)]
-        x_grouped, w_grouped, w_codes, w_scales, sums, activated, pooled, held = {}, {}, {}, {}, {}, {}, {}, {}
+        x_grouped, x_codes, x_scales, w_grouped, w_codes, w_scales = {}, {}, {}, {}, {}, {}
+        sums, passes_done, activated, pooled, held = {}, {}, {}, {}, {}
 
         def round_x(i):
             a, u, t0, t1, cut = X_LOADS[i]
@@ -94,131 +90,172 @@ def tile_picked_pool_lin_gelu_sub_e_kernel(tc, xT, w, b, offs, out):
                     src = x_raw[i][:, :, s0:s1].rearrange("p e t -> p t e")
                     round_to_bf16(nc, engine, pairs[a, u][:, t0 + s0 : t0 + s1, :], src)
 
-        def gather(a, u, parts):
+        def gather(a, u, first=0, end=S):
             window = pairs[a, u][:].rearrange("p t e -> p (t e)").bitcast(U32)
             dense = picked[a][:, u, :, :].rearrange("p s e -> p (s e)").bitcast(U32)
-            for part in parts:
-                part_offsets = offsets[:, part.start // STRIPE : part.stop // STRIPE]
-                nc.vector.tensor_copy(out=dense[:, part], in_=window.indirect(part_offsets))
+            nc.vector.tensor_copy(out=dense[:, first:end], in_=window.indirect(offsets[:, first // STRIPE : end // STRIPE]))
 
-        def weave(a, parts, engine="vector"):
+        def gather_half(a, u, h):
+            gather(a, u, h * HALF, (h + 1) * HALF)
+
+        def weave(a, h):
             if a not in x_grouped:
-                x_grouped[a] = sb([P, S * PACK], BF16, f"x_grouped{a}")
-            dt = I32 if engine == "vector" else U32
-            words = picked[a][:].rearrange("p u s e -> p (u s e)").bitcast(dt).rearrange("p (u s) -> p s u", u=2)
-            side_by_side = x_grouped[a][:].bitcast(dt).rearrange("p (s u) -> p s u", u=2)
-            for part in parts:
-                if engine == "vector":
-                    nc.vector.tensor_copy(out=side_by_side[:, part, :], in_=words[:, part, :])
-                else:
-                    nc.scalar.copy(out=side_by_side[:, part, :], in_=words[:, part, :])
+                x_grouped[a] = sb([P, 2, HALF * PACK], BF16, f"x_grouped{a}")
+            words = picked[a][:].rearrange("p u s e -> p (u s e)").bitcast(I32).rearrange("p (u s) -> p s u", u=2)
+            side_by_side = x_grouped[a][:, h, :].bitcast(I32).rearrange("p (s u) -> p s u", u=2)
+            nc.vector.tensor_copy(out=side_by_side, in_=words[:, h * HALF : (h + 1) * HALF, :])
 
-        def quantise_x(a, parts):
-            for part in parts:
-                nc.vector.quantize_mx(
-                    out=x_codes[a][:, part].bitcast(FP8X4),
-                    scales=x_scales[a][:, part],
-                    in_=x_grouped[a][:, PACK * part.start : PACK * part.stop],
-                )
+        def quantise_x(a, h):
+            x_codes[a, h] = sb([P, HALF], U32, f"x_codes{a}_{h}")
+            x_scales[a, h] = sb([P, HALF], U8, f"x_scales{a}_{h}")
+            nc.vector.quantize_mx(out=x_codes[a, h][:].bitcast(FP8X4), scales=x_scales[a, h][:], in_=x_grouped[a][:, h, :])
 
-        def round_w(i):
-            load, c0, c1, cut = W_PIECES[i]
+        def round_w(name):
+            load, c0, c1, cut = W_PIECES[name]
             first = c0 - W_LOADS[load][1]
-            grouped = sb([P, c1 - c0, PACK], BF16, f"w_grouped{i}")
+            grouped = sb([P, c1 - c0, PACK], BF16, f"w_grouped{name}")
             for engine, s0, s1 in (("scalar", 0, cut), ("vector", cut, c1 - c0)):
                 if s0 < s1:
                     dst = grouped[:, s0:s1, :].rearrange("p (c i) j -> p c j i", i=RUN)
                     src = w_raw[load][:, :, first + s0 : first + s1].rearrange("p j (c i) -> p c j i", i=RUN)
                     round_to_bf16(nc, engine, dst, src)
-            w_grouped[i] = grouped
+            w_grouped[name] = grouped
 
-        def quantise_w(i):
-            load, c0, c1, cut = W_PIECES[i]
-            w_codes[i] = sb([P, c1 - c0], U32, f"w_codes{i}")
-            w_scales[i] = sb([P, c1 - c0], U8, f"w_scales{i}")
+        def quantise_w(name):
+            load, c0, c1, cut = W_PIECES[name]
+            w_codes[name] = sb([P, c1 - c0], U32, f"w_codes{name}")
+            w_scales[name] = sb([P, c1 - c0], U8, f"w_scales{name}")
             nc.vector.quantize_mx(
-                out=w_codes[i][:].bitcast(FP8X4), scales=w_scales[i][:], in_=w_grouped[i][:].rearrange("p c j -> p (c j)")
+                out=w_codes[name][:].bitcast(FP8X4), scales=w_scales[name][:], in_=w_grouped[name][:].rearrange("p c j -> p (c j)")
             )
 
-        def multiply(i, tiles=None):
-            load, c0, c1, cut = W_PIECES[i]
+        def multiply(name):
+            load, c0, c1, cut = W_PIECES[name]
             a = W_LOADS[load][0]
-            for m in tiles or range(c0 // P, c1 // P):
+            for m in range(c0 // P, c1 // P):
                 columns = slice(m * P - c0, (m + 1) * P - c0)
-                for g in GROUPS[m]:
-                    if a == 0:
-                        last = (m, g.stop) == (M_TILES - 1, S)
-                        sums[m, g.start] = psum.tile([P, g.stop - g.start], F32, name=f"sums{m}_{g.start}", tag="spare" if last else f"sums{m}_{g.start}")
+                done = passes_done.get(m, 0)
+                passes_done[m] = done + 1
+                for h in range(2):
+                    if done == 0:
+                        last = (m, h) == (M_TILES - 1, 1)
+                        sums[m, h] = psum.tile([P, HALF], F32, name=f"sums{m}_{h}", tag="spare" if last else f"sums{m}_{h}")
                     nc.tensor.matmul_mx(
-                        out=sums[m, g.start][:],
-                        lhsT=w_codes[i][:, columns].bitcast(FP8X4),
-                        lhsT_scale=w_scales[i][:, columns],
-                        rhs=x_codes[a][:, g].bitcast(FP8X4),
-                        rhs_scale=x_scales[a][:, g],
-                        start=(a == 0),
-                        stop=(a == PASSES - 1),
+                        out=sums[m, h][:],
+                        lhsT=w_codes[name][:, columns].bitcast(FP8X4),
+                        lhsT_scale=w_scales[name][:, columns],
+                        rhs=x_codes[a, h][:].bitcast(FP8X4),
+                        rhs_scale=x_scales[a, h][:],
+                        start=(done == 0),
+                        stop=(done == PASSES - 1),
                     )
 
         def take_bias():
             held["bias"] = sb([P, M_TILES], F32, "bias")
-            nc.vector.tensor_copy(out=held["bias"][:], in_=bias_bank[:, 0:M_TILES])
+            nc.scalar.activation(out=held["bias"][:], in_=bias_bank[:, 0:M_TILES], func=COPY)
 
-        def activate(m, parts=HALVES):
+        def activate(m, h):
             if m not in activated:
-                if m < 2:
-                    if "y01" not in held:
-                        held["y01"] = sb([P, 2, S], F32, "y01")
-                    activated[m] = held["y01"][:, m, :]
-                else:
-                    activated[m] = sb([P, S], F32, f"y{m}")[:]
-            for part in parts:
-                g = [g for g in GROUPS[m] if g.start <= part.start < g.stop][0]
-                src = sums[m, g.start][:, part.start - g.start : part.stop - g.start]
-                nc.scalar.activation(out=activated[m][:, part], in_=src, func=GELU, bias=held["bias"][:, m : m + 1])
+                activated[m] = sb([P, S], F32, f"y{m}")[:]
+            nc.scalar.activation(
+                out=activated[m][:, h * HALF : (h + 1) * HALF], in_=sums[m, h][:], func=GELU, bias=held["bias"][:, m : m + 1]
+            )
 
-        def pool(m, parts=HALVES):
+        def pool(m, first=0, end=S):
             if m not in pooled:
                 pooled[m] = sb([P, V], F32, f"pooled{m}")
-            for part in parts:
-                nc.vector.tensor_reduce(
-                    out=pooled[m][:, part.start // D : part.stop // D],
-                    in_=activated[m][:, part].rearrange("p (v d) -> p v d", d=D),
-                    axis=mybir.AxisListType.X,
-                    op=mybir.AluOpType.max,
-                )
+            nc.vector.tensor_reduce(
+                out=pooled[m][:, first // D : end // D],
+                in_=activated[m][:, first:end].rearrange("p (v d) -> p v d", d=D),
+                axis=mybir.AxisListType.X,
+                op=mybir.AluOpType.max,
+            )
+
+        def pool_half(m, h):
+            pool(m, h * HALF, (h + 1) * HALF)
 
         def store(m):
             nc.sync.dma_start(out=out[m * P : (m + 1) * P, :], in_=pooled[m][:])
 
-        def clock(name, src):
-            tick = keep.tile([P, 1], src.dtype, name=name)
-            nc.gpsimd.tensor_copy(out=tick[:], in_=src)
+        def activate_part(m, first, end):
+            h = first // HALF
+            src = sums[m, h][:, first - h * HALF : end - h * HALF]
+            nc.scalar.activation(out=activated[m][:, first:end], in_=src, func=GELU, bias=held["bias"][:, m : m + 1])
 
-        A, B = HALVES[:1], HALVES[1:]
-        for i in range(len(X_LOADS)):
-            round_x(i)
+        round_x(0)
+        gather(0, 0)
+        round_x(1)
         take_bias()
-        for i in range(len(W_PIECES)):
-            round_w(i)
-        quantise_w(0)
-        for a in range(PASSES - 1):
-            gather(a, 0, WHOLE)
-            gather(a, 1, HALVES)
-        gather(2, 0, WHOLE)
-        gather(2, 1, A)
-        for a in range(PASSES - 1):
-            weave(a, HALVES)
-            quantise_x(a, HALVES)
-        quantise_w(1)
-        gather(2, 1, B)
-        for i in range(2, len(W_PIECES)):
-            quantise_w(i)
-        weave(2, HALVES)
-        quantise_x(2, HALVES)
-        for i in range(len(W_PIECES)):
-            multiply(i)
-        for m in range(M_TILES):
-            activate(m)
-        for m in range(M_TILES):
-            pool(m)
+        gather_half(0, 1, 0)
+        gather_half(0, 1, 1)
+        weave(0, 0)
+        weave(0, 1)
+        quantise_x(0, 0)
+        quantise_x(0, 1)
+        round_x(2)
+        gather(1, 0)
+        round_x(3)
+        round_x(4)
+        gather_half(1, 1, 0)
+        gather_half(1, 1, 1)
+        weave(1, 0)
+        weave(1, 1)
+        quantise_x(1, 0)
+        quantise_x(1, 1)
+        round_x(5)
+        round_x(6)
+        gather(2, 0)
+        round_x(7)
+        round_x(8)
+        gather_half(2, 1, 0)
+        gather_half(2, 1, 1)
+        round_w("A")
+        quantise_w("A")
+        multiply("A")
+        weave(2, 0)
+        weave(2, 1)
+        quantise_x(2, 0)
+        round_w("B0")
+        quantise_w("B0")
+        multiply("B0")
+        round_w("B1")
+        quantise_x(2, 1)
+        round_w("C0")
+        quantise_w("C0")
+        multiply("C0")
+        round_w("C1")
+        quantise_w("B1")
+        multiply("B1")
+        round_w("D")
+        quantise_w("C1")
+        multiply("C1")
+        quantise_w("D")
+        multiply("D")
+        round_w("E")
+        round_w("F")
+        quantise_w("E")
+        multiply("E")
+        quantise_w("F")
+        multiply("F")
+        activate(0, 0)
+        activate(0, 1)
+        round_w("G")
+        round_w("H")
+        quantise_w("G")
+        multiply("G")
+        quantise_w("H")
+        multiply("H")
+        for m in range(1, M_TILES - 1):
+            activate(m, 0)
+            activate(m, 1)
+        activate(3, 0)
+        activate_part(3, 256, 384)
+        activate_part(3, 384, 512)
+        for m in range(M_TILES - 1):
+            pool_half(m, 0)
+            pool_half(m, 1)
             store(m)
+        pool_half(3, 0)
+        pool(3, 256, 384)
+        pool(3, 384, 512)
+        store(3)

@@ -22,13 +22,13 @@ K_PASS = P * PACK
 PASSES = K // K_PASS
 M_TILES = N // P
 STRIPE = 16
-RUN = 4
+RUN = 2
 HALF = S // 2
 
-X_LOADS = [(0, 0, 0, 1024, 352), (0, 1, 0, 1024, 352), (1, 0, 0, 1024, 512), (1, 1, 0, 512, 512), (1, 1, 512, 1024, 512), (2, 0, 0, 512, 512), (2, 0, 512, 1024, 512), (2, 1, 0, 512, 512), (2, 1, 512, 1024, 320)]
+X_LOADS = [(0, 0, 0, 1024, 352), (0, 1, 0, 1024, 352), (1, 0, 0, 1024, 512), (1, 1, 0, 512, 512), (1, 1, 512, 1024, 512), (2, 0, 0, 512, 512), (2, 0, 512, 1024, 512), (2, 1, 0, 576, 576), (2, 1, 576, 1024, 224)]
 W_LOADS = [(0, 0, 256), (1, 0, 256), (2, 0, 256), (0, 256, 512), (1, 256, 384), (2, 256, 384), (1, 384, 512), (2, 384, 512)]
-W_PIECES = {"A": (0, 0, 256, 256), "B0": (1, 0, 128, 128), "B1": (1, 128, 256, 128), "C0": (2, 0, 128, 128), "C1": (2, 128, 256, 128), "D": (3, 256, 512, 128), "E": (4, 256, 384, 128), "F": (5, 256, 384, 0), "G": (6, 384, 512, 128), "H": (7, 384, 512, 0)}
-TAGS = {"x_grouped2": "w_raw0", "x_codes2_1": "w_raw1", "w_codesB1": "w_raw2", "y0": "w_raw3", "y1": "w_groupedF"}
+W_PIECES = {"A0": (0, 0, 128, 128), "A1": (0, 128, 256, 128), "B0": (1, 0, 128, 128), "B1": (1, 128, 256, 128), "C0": (2, 0, 128, 128), "C1": (2, 128, 256, 128), "D": (3, 256, 512, 128), "E": (4, 256, 384, 128), "F": (5, 256, 384, 0), "G": (6, 384, 512, 128), "H": (7, 384, 512, 0)}
+TAGS = {"x_codes1_1": "x_raw7", "x_grouped2": "w_raw0", "x_codes2_1": "w_raw1", "w_codesB1": "w_raw2", "y0": "w_raw3", "y1": "w_groupedF"}
 
 
 def round_to_bf16(nc, engine, dst, src):
@@ -201,17 +201,20 @@ def tile_picked_pool_lin_gelu_sub_e_kernel(tc, xT, w, b, offs, out):
         weave(1, 0)
         weave(1, 1)
         quantise_x(1, 0)
-        quantise_x(1, 1)
         round_x(5)
         round_x(6)
         gather(2, 0)
         round_x(7)
         round_x(8)
+        quantise_x(1, 1)
         gather_half(2, 1, 0)
         gather_half(2, 1, 1)
-        round_w("A")
-        quantise_w("A")
-        multiply("A")
+        round_w("A0")
+        quantise_w("A0")
+        multiply("A0")
+        round_w("A1")
+        quantise_w("A1")
+        multiply("A1")
         weave(2, 0)
         weave(2, 1)
         quantise_x(2, 0)

@@ -22,13 +22,36 @@ K_PASS = P * PACK
 PASSES = K // K_PASS
 M_TILES = N // P
 STRIPE = 16
-RUN = 2
 HALF = S // 2
+QUARTER = S // 4
+RUN = 2
 
-X_LOADS = [(0, 0, 0, 1024, 352), (0, 1, 0, 1024, 352), (1, 0, 0, 1024, 512), (1, 1, 0, 512, 512), (1, 1, 512, 1024, 512), (2, 0, 0, 512, 512), (2, 0, 512, 1024, 512), (2, 1, 0, 576, 576), (2, 1, 576, 1024, 224)]
-W_LOADS = [(0, 0, 256), (1, 0, 256), (2, 0, 256), (0, 256, 512), (1, 256, 384), (2, 256, 384), (1, 384, 512), (2, 384, 512)]
-W_PIECES = {"A0": (0, 0, 128, 128), "A1": (0, 128, 256, 128), "B0": (1, 0, 128, 128), "B1": (1, 128, 256, 128), "C0": (2, 0, 128, 128), "C1": (2, 128, 256, 128), "D": (3, 256, 512, 128), "E": (4, 256, 384, 128), "F": (5, 256, 384, 0), "G": (6, 384, 512, 128), "H": (7, 384, 512, 0)}
-TAGS = {"x_codes1_1": "x_raw7", "x_grouped2": "w_raw0", "x_codes2_1": "w_raw1", "w_codesB1": "w_raw2", "y0": "w_raw3", "y1": "w_groupedF"}
+SCALAR_THIRD = 352
+LAST_CUT = 576
+X_LOADS = [
+    (0, 0, 0, T, SCALAR_THIRD),
+    (0, 1, 0, T, SCALAR_THIRD),
+    (1, 0, 0, T, T // 2),
+    (1, 1, 0, T // 2, T // 2),
+    (1, 1, T // 2, T, T // 2),
+    (2, 0, 0, T // 2, T // 2),
+    (2, 0, T // 2, T, T // 2),
+    (2, 1, 0, LAST_CUT, LAST_CUT),
+    (2, 1, LAST_CUT, T, (T - LAST_CUT) // 2),
+]
+
+W_LOADS = [(0, 0, 2), (1, 0, 2), (2, 0, 2), (0, 2, 4), (1, 2, 3), (2, 2, 3), (1, 3, 4), (2, 3, 4)]
+
+PASS0_OF_TILES_2_3 = (0, 2, 4)
+VECTOR_ROUNDS = {(0, 3), (1, 2), (2, 3)}
+
+REUSED_BUFFERS = {
+    "x_codes1_1": "x_raw7",
+    "x_woven2": "w_raw0",
+    "x_codes2_1": "w_raw1",
+    "w_codes1_1": "w_raw2",
+    "activated1": "w_rounded2_2",
+}
 
 
 def round_to_bf16(nc, engine, dst, src):
@@ -45,7 +68,7 @@ def tile_picked_pool_lin_gelu_sub_e_kernel(tc, xT, w, b, offs, out):
         psum = ctx.enter_context(tc.psum_pool(name="psum", bufs=1))
 
         def sb(shape, dtype, name):
-            return keep.tile(shape, dtype, name=name, tag=TAGS.get(name, name), align_bytes=256)
+            return keep.tile(shape, dtype, name=name, tag=REUSED_BUFFERS.get(name, name), align_bytes=256)
 
         zeros = sb([P, 8], F32, "zeros")
         nc.gpsimd.memset(zeros[:], 0.0)
@@ -59,7 +82,7 @@ def tile_picked_pool_lin_gelu_sub_e_kernel(tc, xT, w, b, offs, out):
 
         offsets = keep.tile([P, S // STRIPE], U16, name="offsets")
         x_raw = []
-        for i, (a, u, t0, t1, cut) in enumerate(X_LOADS):
+        for i, (a, u, t0, t1, scalar_nodes) in enumerate(X_LOADS):
             rows = xT[a * K_PASS : (a + 1) * K_PASS, :].rearrange("(p j) t -> p j t", j=PACK)
             raw = sb([P, 2, t1 - t0], F32, f"x_raw{i}")
             nc.sync.dma_start(out=raw[:], in_=rows[:, 2 * u : 2 * u + 2, t0:t1])
@@ -68,100 +91,98 @@ def tile_picked_pool_lin_gelu_sub_e_kernel(tc, xT, w, b, offs, out):
                 nc.sync.dma_start(offsets[:], offs)
             if i == 1:
                 nc.sync.dma_start(out=bias_rows[0:M_TILES, :], in_=b.rearrange("(m p) o -> m (p o)", p=P))
-        w_raw = []
-        for i, (a, c0, c1) in enumerate(W_LOADS):
+        w_raw = {}
+        for i, (a, m0, m1) in enumerate(W_LOADS):
             rows = w[a * K_PASS : (a + 1) * K_PASS, :].rearrange("(p j) c -> p j c", j=PACK)
-            raw = sb([P, PACK, c1 - c0], F32, f"w_raw{i}")
-            nc.sync.dma_start(out=raw[:], in_=rows[:, :, c0:c1])
-            w_raw.append(raw)
+            raw = sb([P, PACK, (m1 - m0) * P], F32, f"w_raw{i}")
+            nc.sync.dma_start(out=raw[:], in_=rows[:, :, m0 * P : m1 * P])
+            for m in range(m0, m1):
+                w_raw[a, m] = raw[:, :, (m - m0) * P : (m - m0 + 1) * P]
 
-        bias_bank = psum.tile([P, P], F32, name="bias_bank", tag="spare")
+        bias_bank = psum.tile([P, P], F32, name="bias_bank", tag="bias_then_last_sums")
         nc.tensor.transpose(bias_bank[:], bias_rows[:], identity[:])
 
         pairs = {(a, u): sb([P, T, 2], BF16, f"pairs{a}_{u}") for a in range(PASSES) for u in range(2)}
         picked = [sb([P, 2, S, 2], BF16, f"picked{a}") for a in range(PASSES)]
-        x_grouped, x_codes, x_scales, w_grouped, w_codes, w_scales = {}, {}, {}, {}, {}, {}
-        sums, passes_done, activated, pooled, held = {}, {}, {}, {}, {}
+        x_woven, x_codes, x_scales = {}, {}, {}
+        w_rounded, w_codes, w_scales = {}, {}, {}
+        sums, activated, pooled = {}, {}, {}
 
         def round_x(i):
-            a, u, t0, t1, cut = X_LOADS[i]
-            for engine, s0, s1 in (("scalar", 0, cut), ("vector", cut, t1 - t0)):
+            a, u, t0, t1, scalar_nodes = X_LOADS[i]
+            for engine, s0, s1 in (("scalar", 0, scalar_nodes), ("vector", scalar_nodes, t1 - t0)):
                 if s0 < s1:
                     src = x_raw[i][:, :, s0:s1].rearrange("p e t -> p t e")
                     round_to_bf16(nc, engine, pairs[a, u][:, t0 + s0 : t0 + s1, :], src)
 
-        def gather(a, u, first=0, end=S):
+        def gather(a, u, first, end):
             window = pairs[a, u][:].rearrange("p t e -> p (t e)").bitcast(U32)
             dense = picked[a][:, u, :, :].rearrange("p s e -> p (s e)").bitcast(U32)
             nc.vector.tensor_copy(out=dense[:, first:end], in_=window.indirect(offsets[:, first // STRIPE : end // STRIPE]))
 
-        def gather_half(a, u, h):
-            gather(a, u, h * HALF, (h + 1) * HALF)
+        def gather_in_halves(a, u):
+            for h in range(2):
+                gather(a, u, h * HALF, (h + 1) * HALF)
 
-        def weave(a, h):
-            if a not in x_grouped:
-                x_grouped[a] = sb([P, 2, HALF * PACK], BF16, f"x_grouped{a}")
+        def weave(a):
+            x_woven[a] = sb([P, 2, HALF * PACK], BF16, f"x_woven{a}")
             words = picked[a][:].rearrange("p u s e -> p (u s e)").bitcast(I32).rearrange("p (u s) -> p s u", u=2)
-            side_by_side = x_grouped[a][:, h, :].bitcast(I32).rearrange("p (s u) -> p s u", u=2)
-            nc.vector.tensor_copy(out=side_by_side, in_=words[:, h * HALF : (h + 1) * HALF, :])
+            for h in range(2):
+                side_by_side = x_woven[a][:, h, :].bitcast(I32).rearrange("p (s u) -> p s u", u=2)
+                nc.vector.tensor_copy(out=side_by_side, in_=words[:, h * HALF : (h + 1) * HALF, :])
 
         def quantise_x(a, h):
             x_codes[a, h] = sb([P, HALF], U32, f"x_codes{a}_{h}")
             x_scales[a, h] = sb([P, HALF], U8, f"x_scales{a}_{h}")
-            nc.vector.quantize_mx(out=x_codes[a, h][:].bitcast(FP8X4), scales=x_scales[a, h][:], in_=x_grouped[a][:, h, :])
+            nc.vector.quantize_mx(out=x_codes[a, h][:].bitcast(FP8X4), scales=x_scales[a, h][:], in_=x_woven[a][:, h, :])
 
-        def round_w(name):
-            load, c0, c1, cut = W_PIECES[name]
-            first = c0 - W_LOADS[load][1]
-            grouped = sb([P, c1 - c0, PACK], BF16, f"w_grouped{name}")
-            for engine, s0, s1 in (("scalar", 0, cut), ("vector", cut, c1 - c0)):
-                if s0 < s1:
-                    dst = grouped[:, s0:s1, :].rearrange("p (c i) j -> p c j i", i=RUN)
-                    src = w_raw[load][:, :, first + s0 : first + s1].rearrange("p j (c i) -> p c j i", i=RUN)
-                    round_to_bf16(nc, engine, dst, src)
-            w_grouped[name] = grouped
+        def round_w(a, m0, m1):
+            rounded = sb([P, (m1 - m0) * P, PACK], BF16, f"w_rounded{a}_{m0}")
+            for m in range(m0, m1):
+                engine = "vector" if (a, m) in VECTOR_ROUNDS else "scalar"
+                dst = rounded[:, (m - m0) * P : (m - m0 + 1) * P, :].rearrange("p (c i) j -> p c j i", i=RUN)
+                round_to_bf16(nc, engine, dst, w_raw[a, m].rearrange("p j (c i) -> p c j i", i=RUN))
+            w_rounded[a, m0] = rounded
 
-        def quantise_w(name):
-            load, c0, c1, cut = W_PIECES[name]
-            w_codes[name] = sb([P, c1 - c0], U32, f"w_codes{name}")
-            w_scales[name] = sb([P, c1 - c0], U8, f"w_scales{name}")
+        def quantise_w(a, m0, m1):
+            w_codes[a, m0] = sb([P, (m1 - m0) * P], U32, f"w_codes{a}_{m0}")
+            w_scales[a, m0] = sb([P, (m1 - m0) * P], U8, f"w_scales{a}_{m0}")
             nc.vector.quantize_mx(
-                out=w_codes[name][:].bitcast(FP8X4), scales=w_scales[name][:], in_=w_grouped[name][:].rearrange("p c j -> p (c j)")
+                out=w_codes[a, m0][:].bitcast(FP8X4),
+                scales=w_scales[a, m0][:],
+                in_=w_rounded[a, m0][:].rearrange("p c j -> p (c j)"),
             )
 
-        def multiply(name):
-            load, c0, c1, cut = W_PIECES[name]
-            a = W_LOADS[load][0]
-            for m in range(c0 // P, c1 // P):
-                columns = slice(m * P - c0, (m + 1) * P - c0)
-                done = passes_done.get(m, 0)
-                passes_done[m] = done + 1
+        def multiply(a, m0, m1):
+            for m in range(m0, m1):
+                columns = slice((m - m0) * P, (m - m0 + 1) * P)
                 for h in range(2):
-                    if done == 0:
+                    if a == 0:
                         last = (m, h) == (M_TILES - 1, 1)
-                        sums[m, h] = psum.tile([P, HALF], F32, name=f"sums{m}_{h}", tag="spare" if last else f"sums{m}_{h}")
+                        tag = "bias_then_last_sums" if last else f"sums{m}_{h}"
+                        sums[m, h] = psum.tile([P, HALF], F32, name=f"sums{m}_{h}", tag=tag)
                     nc.tensor.matmul_mx(
                         out=sums[m, h][:],
-                        lhsT=w_codes[name][:, columns].bitcast(FP8X4),
-                        lhsT_scale=w_scales[name][:, columns],
+                        lhsT=w_codes[a, m0][:, columns].bitcast(FP8X4),
+                        lhsT_scale=w_scales[a, m0][:, columns],
                         rhs=x_codes[a, h][:].bitcast(FP8X4),
                         rhs_scale=x_scales[a, h][:],
-                        start=(done == 0),
-                        stop=(done == PASSES - 1),
+                        start=(a == 0),
+                        stop=(a == PASSES - 1),
                     )
 
-        def take_bias():
-            held["bias"] = sb([P, M_TILES], F32, "bias")
-            nc.scalar.activation(out=held["bias"][:], in_=bias_bank[:, 0:M_TILES], func=COPY)
+        def quantise_and_multiply(a, m0, m1):
+            quantise_w(a, m0, m1)
+            multiply(a, m0, m1)
 
-        def activate(m, h):
+        def activate(m, first, end):
             if m not in activated:
-                activated[m] = sb([P, S], F32, f"y{m}")[:]
-            nc.scalar.activation(
-                out=activated[m][:, h * HALF : (h + 1) * HALF], in_=sums[m, h][:], func=GELU, bias=held["bias"][:, m : m + 1]
-            )
+                activated[m] = sb([P, S], F32, f"activated{m}")
+            h = first // HALF
+            src = sums[m, h][:, first - h * HALF : end - h * HALF]
+            nc.scalar.activation(out=activated[m][:, first:end], in_=src, func=GELU, bias=bias[:, m : m + 1])
 
-        def pool(m, first=0, end=S):
+        def pool(m, first, end):
             if m not in pooled:
                 pooled[m] = sb([P, V], F32, f"pooled{m}")
             nc.vector.tensor_reduce(
@@ -171,94 +192,66 @@ def tile_picked_pool_lin_gelu_sub_e_kernel(tc, xT, w, b, offs, out):
                 op=mybir.AluOpType.max,
             )
 
-        def pool_half(m, h):
-            pool(m, h * HALF, (h + 1) * HALF)
-
-        def store(m):
-            nc.sync.dma_start(out=out[m * P : (m + 1) * P, :], in_=pooled[m][:])
-
-        def activate_part(m, first, end):
-            h = first // HALF
-            src = sums[m, h][:, first - h * HALF : end - h * HALF]
-            nc.scalar.activation(out=activated[m][:, first:end], in_=src, func=GELU, bias=held["bias"][:, m : m + 1])
+        parts = {m: [(0, HALF), (HALF, S)] for m in range(M_TILES - 1)}
+        parts[M_TILES - 1] = [(0, HALF), (HALF, HALF + QUARTER), (HALF + QUARTER, S)]
 
         round_x(0)
-        gather(0, 0)
+        gather(0, 0, 0, S)
         round_x(1)
-        take_bias()
-        gather_half(0, 1, 0)
-        gather_half(0, 1, 1)
-        weave(0, 0)
-        weave(0, 1)
+        bias = sb([P, M_TILES], F32, "bias")
+        nc.scalar.activation(out=bias[:], in_=bias_bank[:, 0:M_TILES], func=COPY)
+        gather_in_halves(0, 1)
+        weave(0)
         quantise_x(0, 0)
         quantise_x(0, 1)
+
         round_x(2)
-        gather(1, 0)
+        gather(1, 0, 0, S)
         round_x(3)
         round_x(4)
-        gather_half(1, 1, 0)
-        gather_half(1, 1, 1)
-        weave(1, 0)
-        weave(1, 1)
+        gather_in_halves(1, 1)
+        weave(1)
         quantise_x(1, 0)
+
         round_x(5)
         round_x(6)
-        gather(2, 0)
+        gather(2, 0, 0, S)
         round_x(7)
         round_x(8)
         quantise_x(1, 1)
-        gather_half(2, 1, 0)
-        gather_half(2, 1, 1)
-        round_w("A0")
-        quantise_w("A0")
-        multiply("A0")
-        round_w("A1")
-        quantise_w("A1")
-        multiply("A1")
-        weave(2, 0)
-        weave(2, 1)
+        gather_in_halves(2, 1)
+        for m in range(2):
+            round_w(0, m, m + 1)
+            quantise_and_multiply(0, m, m + 1)
+        weave(2)
         quantise_x(2, 0)
-        round_w("B0")
-        quantise_w("B0")
-        multiply("B0")
-        round_w("B1")
+        round_w(1, 0, 1)
+        quantise_and_multiply(1, 0, 1)
+        round_w(1, 1, 2)
         quantise_x(2, 1)
-        round_w("C0")
-        quantise_w("C0")
-        multiply("C0")
-        round_w("C1")
-        quantise_w("B1")
-        multiply("B1")
-        round_w("D")
-        quantise_w("C1")
-        multiply("C1")
-        quantise_w("D")
-        multiply("D")
-        round_w("E")
-        round_w("F")
-        quantise_w("E")
-        multiply("E")
-        quantise_w("F")
-        multiply("F")
-        activate(0, 0)
-        activate(0, 1)
-        round_w("G")
-        round_w("H")
-        quantise_w("G")
-        multiply("G")
-        quantise_w("H")
-        multiply("H")
-        for m in range(1, M_TILES - 1):
-            activate(m, 0)
-            activate(m, 1)
-        activate(3, 0)
-        activate_part(3, 256, 384)
-        activate_part(3, 384, 512)
-        for m in range(M_TILES - 1):
-            pool_half(m, 0)
-            pool_half(m, 1)
-            store(m)
-        pool_half(3, 0)
-        pool(3, 256, 384)
-        pool(3, 384, 512)
-        store(3)
+        round_w(2, 0, 1)
+        quantise_and_multiply(2, 0, 1)
+        round_w(2, 1, 2)
+        quantise_and_multiply(1, 1, 2)
+        round_w(*PASS0_OF_TILES_2_3)
+        quantise_and_multiply(2, 1, 2)
+
+        round_w(1, 2, 3)
+        quantise_and_multiply(*PASS0_OF_TILES_2_3)
+        quantise_and_multiply(1, 2, 3)
+        for first, end in parts[0]:
+            activate(0, first, end)
+        round_w(2, 2, 3)
+        quantise_and_multiply(2, 2, 3)
+        round_w(1, 3, 4)
+        round_w(2, 3, 4)
+        quantise_and_multiply(1, 3, 4)
+        quantise_and_multiply(2, 3, 4)
+
+        for m in range(1, M_TILES):
+            for first, end in parts[m]:
+                activate(m, first, end)
+        for m in range(M_TILES):
+            for first, end in parts[m]:
+                pool(m, first, end)
+            nc.sync.dma_start(out=out[m * P : (m + 1) * P, :], in_=pooled[m][:])

@@ -34,11 +34,13 @@ X_LOADS = [
     (1, 0, 0, T, T // 2),
     (1, 1, 0, T // 2, T // 2),
     (1, 1, T // 2, T, T // 2),
-    (2, 0, 0, T // 2, T // 2),
-    (2, 0, T // 2, T, T // 2),
-    (2, 1, 0, LAST_CUT, LAST_CUT),
+    (2, 0, 0, T, 0),
+    (2, 0, 0, T, 0),
+    (2, 1, 0, LAST_CUT, LAST_CUT - QUARTER),
     (2, 1, LAST_CUT, T, (T - LAST_CUT) // 2),
 ]
+
+ROW_LOADS = {5: 0, 6: 1}
 
 W_LOADS = [(0, 0, 2), (1, 0, 2), (2, 0, 2), (0, 2, 4), (1, 2, 3), (2, 2, 3), (1, 3, 4), (2, 3, 4)]
 
@@ -84,8 +86,12 @@ def tile_picked_pool_lin_gelu_sub_e_kernel(tc, xT, w, b, offs, out):
         x_raw = []
         for i, (a, u, t0, t1, scalar_nodes) in enumerate(X_LOADS):
             rows = xT[a * K_PASS : (a + 1) * K_PASS, :].rearrange("(p j) t -> p j t", j=PACK)
-            raw = sb([P, 2, t1 - t0], F32, f"x_raw{i}")
-            nc.sync.dma_start(out=raw[:], in_=rows[:, 2 * u : 2 * u + 2, t0:t1])
+            if i in ROW_LOADS:
+                raw = sb([P, T], F32, f"x_raw{i}")
+                nc.sync.dma_start(out=raw[:], in_=rows[:, ROW_LOADS[i], :])
+            else:
+                raw = sb([P, 2, t1 - t0], F32, f"x_raw{i}")
+                nc.sync.dma_start(out=raw[:], in_=rows[:, 2 * u : 2 * u + 2, t0:t1])
             x_raw.append(raw)
             if i == 0:
                 nc.sync.dma_start(offsets[:], offs)
@@ -102,7 +108,7 @@ def tile_picked_pool_lin_gelu_sub_e_kernel(tc, xT, w, b, offs, out):
         bias_bank = psum.tile([P, P], F32, name="bias_bank", tag="bias_then_last_sums")
         nc.tensor.transpose(bias_bank[:], bias_rows[:], identity[:])
 
-        pairs = {(a, u): sb([P, T, 2], BF16, f"pairs{a}_{u}") for a in range(PASSES) for u in range(2)}
+        pairs = {(a, u): sb([P, T, 2], BF16, f"pairs{a}_{u}") for a in range(PASSES) for u in range(2) if (a, u) != (2, 0)}
         picked = [sb([P, 2, S, 2], BF16, f"picked{a}") for a in range(PASSES)]
         x_woven, x_codes, x_scales = {}, {}, {}
         w_rounded, w_codes, w_scales = {}, {}, {}
@@ -213,10 +219,11 @@ def tile_picked_pool_lin_gelu_sub_e_kernel(tc, xT, w, b, offs, out):
         weave(1)
         quantise_x(1, 0)
 
-        round_x(5)
-        round_x(6)
-        gather(2, 0, 0, S)
+        picked_rows = sb([P, 2, S], F32, "picked_rows")
+        for i, j in ROW_LOADS.items():
+            nc.scalar.activation(out=picked_rows[:, j, :], in_=x_raw[i][:].indirect(offsets[:]), func=COPY)
         round_x(7)
+        nc.vector.tensor_copy(out=picked[2][:, 0, :, :], in_=picked_rows[:].rearrange("p e s -> p s e"))
         round_x(8)
         quantise_x(1, 1)
         gather_in_halves(2, 1)

@@ -70,7 +70,9 @@ def tile_picked_pool_lin_gelu_sub_e_kernel(tc, xT, w, b, offs, out):
         psum = ctx.enter_context(tc.psum_pool(name="psum", bufs=1))
 
         def sb(shape, dtype, name):
-            return keep.tile(shape, dtype, name=name, tag=REUSED_BUFFERS.get(name, name), align_bytes=256)
+            tag = REUSED_BUFFERS.get(name, name)
+            align = 2048 if tag.startswith(("x_raw", "w_raw")) else 256
+            return keep.tile(shape, dtype, name=name, tag=tag, align_bytes=align)
 
         zeros = sb([P, 8], F32, "zeros")
         nc.gpsimd.memset(zeros[:], 0.0)

from contextlib import ExitStack

import concourse.mybir as mybir
from concourse.masks import make_identity

K, T, D, S, V, N = 1536, 1024, 16, 512, 32, 512
FLOPS = 2 * K * N * S

F32 = mybir.dt.float32
BF16 = mybir.dt.bfloat16
U32 = mybir.dt.uint32
I32 = mybir.dt.int32
U16 = mybir.dt.uint16
U8 = mybir.dt.uint8
FP8X4 = mybir.dt.float8_e4m3fn_x4
COPY = mybir.ActivationFunctionType.Copy
GELU = mybir.ActivationFunctionType.Gelu_apprx_tanh

P = 128
PACK = 4
K_PASS = P * PACK
PASSES = K // K_PASS
M_TILES = N // P
STRIPE = 16
HALF = S // 2
QUARTER = S // 4
RUN = 2

SCALAR_THIRD = 352
LAST_CUT = 576
X_LOADS = [
    (0, 0, 0, T, SCALAR_THIRD),
    (0, 1, 0, T, SCALAR_THIRD),
    (1, 0, 0, T, T // 2),
    (1, 1, 0, T // 2, T // 2),
    (1, 1, T // 2, T, T // 2),
    (2, 0, 0, T, 0),
    (2, 0, 0, T, 0),
    (2, 1, 0, LAST_CUT, LAST_CUT - QUARTER),
    (2, 1, LAST_CUT, T, (T - LAST_CUT) // 2),
]

ROW_LOADS = {5: 0, 6: 1}

W_LOADS = [(0, 0, 2), (1, 0, 2), (2, 0, 2), (0, 2, 4), (1, 2, 3), (2, 2, 3), (1, 3, 4), (2, 3, 4)]

PASS0_OF_TILES_2_3 = (0, 2, 4)
VECTOR_ROUNDS = {(0, 3), (1, 2), (2, 3)}

REUSED_BUFFERS = {
    "x_codes1_1": "x_raw7",
    "x_woven2": "w_raw0",
    "x_codes2_1": "w_raw1",
    "w_codes1_1": "w_raw2",
    "activated1": "w_rounded2_2",
}


def round_to_bf16(nc, engine, dst, src):
    if engine == "scalar":
        nc.scalar.activation(out=dst, in_=src, func=COPY)
    else:
        nc.vector.tensor_copy(out=dst, in_=src)


def tile_picked_pool_lin_gelu_sub_e_kernel(tc, xT, w, b, offs, out):
    nc = tc.nc
    with ExitStack() as ctx:
        keep = ctx.enter_context(tc.tile_pool(name="keep", bufs=1))
        psum = ctx.enter_context(tc.psum_pool(name="psum", bufs=1))

        def sb(shape, dtype, name):
            tag = REUSED_BUFFERS.get(name, name)
            align = 2048 if tag.startswith(("x_raw", "w_raw")) else 256
            return keep.tile(shape, dtype, name=name, tag=tag, align_bytes=align)

        zeros = sb([P, 8], F32, "zeros")
        nc.gpsimd.memset(zeros[:], 0.0)
        gelu_of_zeros = sb([P, 8], F32, "gelu_of_zeros")
        nc.scalar.activation(out=gelu_of_zeros[:], in_=zeros[:], func=GELU)

        identity = sb([P, P], F32, "identity")
        make_identity(nc, identity[:])
        bias_rows = sb([P, P], F32, "bias_rows")
        nc.gpsimd.memset(bias_rows[:], 0.0)

        offsets = keep.tile([P, S // STRIPE], U16, name="offsets")
        x_raw = []
        for i, (a, u, t0, t1, scalar_nodes) in enumerate(X_LOADS):
            rows = xT[a * K_PASS : (a + 1) * K_PASS, :].rearrange("(p j) t -> p j t", j=PACK)
            if i in ROW_LOADS:
                raw = sb([P, T], F32, f"x_raw{i}")
                nc.sync.dma_start(out=raw[:], in_=rows[:, ROW_LOADS[i], :])
            else:
                raw = sb([P, 2, t1 - t0], F32, f"x_raw{i}")
                nc.sync.dma_start(out=raw[:], in_=rows[:, 2 * u : 2 * u + 2, t0:t1])
            x_raw.append(raw)
            if i == 0:
                nc.sync.dma_start(offsets[:], offs)
            if i == 1:
                nc.sync.dma_start(out=bias_rows[0:M_TILES, :], in_=b.rearrange("(m p) o -> m (p o)", p=P))
        w_raw = {}
        for i, (a, m0, m1) in enumerate(W_LOADS):
            rows = w[a * K_PASS : (a + 1) * K_PASS, :].rearrange("(p j) c -> p j c", j=PACK)
            raw = sb([P, PACK, (m1 - m0) * P], F32, f"w_raw{i}")
            nc.sync.dma_start(out=raw[:], in_=rows[:, :, m0 * P : m1 * P])
            for m in range(m0, m1):
                w_raw[a, m] = raw[:, :, (m - m0) * P : (m - m0 + 1) * P]

        bias_bank = psum.tile([P, P], F32, name="bias_bank", tag="bias_then_last_sums")
        nc.tensor.transpose(bias_bank[:], bias_rows[:], identity[:])

        pairs = {(a, u): sb([P, T, 2], BF16, f"pairs{a}_{u}") for a in range(PASSES) for u in range(2) if (a, u) != (2, 0)}
        picked = [sb([P, 2, S, 2], BF16, f"picked{a}") for a in range(PASSES)]
        x_woven, x_codes, x_scales = {}, {}, {}
        w_rounded, w_codes, w_scales = {}, {}, {}
        sums, activated, pooled = {}, {}, {}

        def round_x(i):
            a, u, t0, t1, scalar_nodes = X_LOADS[i]
            for engine, s0, s1 in (("scalar", 0, scalar_nodes), ("vector", scalar_nodes, t1 - t0)):
                if s0 < s1:
                    src = x_raw[i][:, :, s0:s1].rearrange("p e t -> p t e")
                    round_to_bf16(nc, engine, pairs[a, u][:, t0 + s0 : t0 + s1, :], src)

        def gather(a, u, first, end):
            window = pairs[a, u][:].rearrange("p t e -> p (t e)").bitcast(U32)
            dense = picked[a][:, u, :, :].rearrange("p s e -> p (s e)").bitcast(U32)
            nc.vector.tensor_copy(out=dense[:, first:end], in_=window.indirect(offsets[:, first // STRIPE : end // STRIPE]))

        def gather_in_halves(a, u):
            for h in range(2):
                gather(a, u, h * HALF, (h + 1) * HALF)

        def weave(a):
            x_woven[a] = sb([P, 2, HALF * PACK], BF16, f"x_woven{a}")
            words = picked[a][:].rearrange("p u s e -> p (u s e)").bitcast(I32).rearrange("p (u s) -> p s u", u=2)
            for h in range(2):
                side_by_side = x_woven[a][:, h, :].bitcast(I32).rearrange("p (s u) -> p s u", u=2)
                nc.vector.tensor_copy(out=side_by_side, in_=words[:, h * HALF : (h + 1) * HALF, :])

        def quantise_x(a, h):
            x_codes[a, h] = sb([P, HALF], U32, f"x_codes{a}_{h}")
            x_scales[a, h] = sb([P, HALF], U8, f"x_scales{a}_{h}")
            nc.vector.quantize_mx(out=x_codes[a, h][:].bitcast(FP8X4), scales=x_scales[a, h][:], in_=x_woven[a][:, h, :])

        def round_w(a, m0, m1):
            rounded = sb([P, (m1 - m0) * P, PACK], BF16, f"w_rounded{a}_{m0}")
            for m in range(m0, m1):
                engine = "vector" if (a, m) in VECTOR_ROUNDS else "scalar"
                dst = rounded[:, (m - m0) * P : (m - m0 + 1) * P, :].rearrange("p (c i) j -> p c j i", i=RUN)
                round_to_bf16(nc, engine, dst, w_raw[a, m].rearrange("p j (c i) -> p c j i", i=RUN))
            w_rounded[a, m0] = rounded

        def quantise_w(a, m0, m1):
            w_codes[a, m0] = sb([P, (m1 - m0) * P], U32, f"w_codes{a}_{m0}")
            w_scales[a, m0] = sb([P, (m1 - m0) * P], U8, f"w_scales{a}_{m0}")
            nc.vector.quantize_mx(
                out=w_codes[a, m0][:].bitcast(FP8X4),
                scales=w_scales[a, m0][:],
                in_=w_rounded[a, m0][:].rearrange("p c j -> p (c j)"),
            )

        def multiply(a, m0, m1):
            for m in range(m0, m1):
                columns = slice((m - m0) * P, (m - m0 + 1) * P)
                for h in range(2):
                    if a == 0:
                        last = (m, h) == (M_TILES - 1, 1)
                        tag = "bias_then_last_sums" if last else f"sums{m}_{h}"
                        sums[m, h] = psum.tile([P, HALF], F32, name=f"sums{m}_{h}", tag=tag)
                    nc.tensor.matmul_mx(
                        out=sums[m, h][:],
                        lhsT=w_codes[a, m0][:, columns].bitcast(FP8X4),
                        lhsT_scale=w_scales[a, m0][:, columns],
                        rhs=x_codes[a, h][:].bitcast(FP8X4),
                        rhs_scale=x_scales[a, h][:],
                        start=(a == 0),
                        stop=(a == PASSES - 1),
                    )

        def quantise_and_multiply(a, m0, m1):
            quantise_w(a, m0, m1)
            multiply(a, m0, m1)

        def activate(m, first, end):
            if m not in activated:
                activated[m] = sb([P, S], F32, f"activated{m}")
            h = first // HALF
            src = sums[m, h][:, first - h * HALF : end - h * HALF]
            nc.scalar.activation(out=activated[m][:, first:end], in_=src, func=GELU, bias=bias[:, m : m + 1])

        def pool(m, first, end):
            if m not in pooled:
                pooled[m] = sb([P, V], F32, f"pooled{m}")
            nc.vector.tensor_reduce(
                out=pooled[m][:, first // D : end // D],
                in_=activated[m][:, first:end].rearrange("p (v d) -> p v d", d=D),
                axis=mybir.AxisListType.X,
                op=mybir.AluOpType.max,
            )

        parts = {m: [(0, HALF), (HALF, S)] for m in range(M_TILES - 1)}
        parts[M_TILES - 1] = [(0, HALF), (HALF, HALF + QUARTER), (HALF + QUARTER, S)]

        round_x(0)
        gather(0, 0, 0, S)
        round_x(1)
        bias = sb([P, M_TILES], F32, "bias")
        nc.scalar.activation(out=bias[:], in_=bias_bank[:, 0:M_TILES], func=COPY)
        gather_in_halves(0, 1)
        weave(0)
        quantise_x(0, 0)
        quantise_x(0, 1)

        round_x(2)
        gather(1, 0, 0, S)
        round_x(3)
        round_x(4)
        gather_in_halves(1, 1)
        weave(1)
        quantise_x(1, 0)

        picked_rows = sb([P, 2, S], F32, "picked_rows")
        for i, j in ROW_LOADS.items():
            nc.scalar.activation(out=picked_rows[:, j, :], in_=x_raw[i][:].indirect(offsets[:]), func=COPY)
        round_x(7)
        nc.vector.tensor_copy(out=picked[2][:, 0, :, :], in_=picked_rows[:].rearrange("p e s -> p s e"))
        round_x(8)
        quantise_x(1, 1)
        gather_in_halves(2, 1)
        for m in range(2):
            round_w(0, m, m + 1)
            quantise_and_multiply(0, m, m + 1)
        weave(2)
        quantise_x(2, 0)
        round_w(1, 0, 1)
        quantise_and_multiply(1, 0, 1)
        round_w(1, 1, 2)
        quantise_x(2, 1)
        round_w(2, 0, 1)
        quantise_and_multiply(2, 0, 1)
        round_w(2, 1, 2)
        quantise_and_multiply(1, 1, 2)
        round_w(*PASS0_OF_TILES_2_3)
        quantise_and_multiply(2, 1, 2)

        round_w(1, 2, 3)
        quantise_and_multiply(*PASS0_OF_TILES_2_3)
        quantise_and_multiply(1, 2, 3)
        for first, end in parts[0]:
            activate(0, first, end)
        round_w(2, 2, 3)
        quantise_and_multiply(2, 2, 3)
        round_w(1, 3, 4)
        round_w(2, 3, 4)
        quantise_and_multiply(1, 3, 4)
        quantise_and_multiply(2, 3, 4)

        for m in range(1, M_TILES):
            for first, end in parts[m]:
                activate(m, first, end)
        for m in range(M_TILES):
            for first, end in parts[m]:
                pool(m, first, end)
            nc.sync.dma_start(out=out[m * P : (m + 1) * P, :], in_=pooled[m][:])
